import numpy as np, ml_dtypes
CORES = [13,21,141,149]
N = 4
BF = ml_dtypes.bfloat16
W, A, S, CAP, RO = 2048, 512, 2, 128, 4
P, BL = A // S, W // CAP
WT = 2 * np.arange(16) + 1
def counts(rng, fat):
    return np.where(fat, rng.integers(9, 17, fat.shape), rng.integers(0, 9, fat.shape))
def cols(rng, n, top):
    on = np.argsort(rng.random((N, 8, 16, W)), axis=2) < n[:, :, None, :]
    return np.where(on, 1 + (top * rng.random((N, 8, 16, W))).astype(np.int64), 0)
def lines(rng, fat, share):
    o = np.argsort(np.where(fat, 0.0, 1.0) + 0.5 * rng.random((N, 8, W)), axis=-1); nf = np.add.reduce(fat.astype(np.int64), axis=-1)[:, :, None, None]
    v = rng.random((N, 8, 16, A))
    k = np.where(rng.random((N, 8, 16, A)) < share, (v * nf).astype(np.int64), nf + (v * (W - nf)).astype(np.int64))
    return np.take_along_axis(o, k.reshape(N, 8, 16 * A), 2).reshape(N, 8, 16, A)
def hop(e, u):
    return (((e * u) >> 5) + e) & (W - 1)
def first(X):
    u = np.add.reduce(X * WT.reshape(1, 1, 16, 1), axis=2) & (W - 1); h = hop(np.arange(W).reshape(1, 1, W), u)
    y = np.take_along_axis(X, h[:, :, None, :], 3)
    return np.add.reduce(np.sign(y - X), axis=2), np.add.reduce((X > 0).astype(np.int64), axis=2)
def top16(s):
    v = np.full(16, 255); d = (65280 - s) & (W - 1)
    for w in range(15, -1, -1):
        c = min(254, d // (2 * w + 1)); v[w] -= c; d -= c * (2 * w + 1)
    return v
def pack(X, E, M):
    return {"xt": X.reshape(N, 128, W).astype(np.float32).astype(BF), "led": E.reshape(N, 128, A).astype(np.int32), "mk": M.reshape(N, 128, A).astype(np.float32).astype(BF)}
def setup_inputs(rng):
    fat = rng.random((N, 8, W)) < rng.choice(np.array([0.3, 0.5, 0.7]), (N, 8, 1))
    X = cols(rng, counts(rng, fat), 255)
    share = rng.choice(np.array([0.01, 0.05, 0.15, 0.6]), (N, 8, 1, A)) * rng.choice(np.array([0.2, 1.0, 1.5]), (N, 8, 1, 1))
    return pack(X, lines(rng, fat, share), rng.integers(0, 2, (N, 8, 16, A)))
def setup_inputs_spread(rng):
    fat = rng.random((N, 8, W)) < rng.choice(np.array([0.2, 0.5, 0.8]), (N, 8, 1))
    top = np.minimum(np.exp2(8 * rng.random((N, 8, 1, W))).astype(np.int64), 255)
    X = cols(rng, counts(rng, fat), top)
    E = lines(rng, fat, rng.choice(np.array([0.01, 0.05, 0.2, 0.7]), (N, 8, 1, A)))
    low = (W * rng.random((N, 8, 16, A)) ** 4).astype(np.int64); E = np.where(rng.random((N, 8, 1, A)) < 0.25, low, E)
    return pack(X, E, (rng.random((N, 8, 16, A)) < rng.random((N, 8, 1, A))).astype(np.int64))
def setup_inputs_ends(rng):
    kind = rng.integers(0, 3, (N, 8, 1, W))
    X = np.where(kind == 0, 0, np.where(kind == 1, 255, 255 * rng.integers(0, 2, (N, 8, 16, W))))
    X[..., 1] = 1; X[..., hop(1, 256)] = 255
    X[..., 2] = 255; X[..., hop(2, 65280 & (W - 1))] = 0
    X[..., W - 2] = 254; X[..., hop(W - 2, 65024 & (W - 1))] = 255
    X[..., W - 1] = top16(W - 1); X[..., hop(W - 1, W - 1)] = 0
    sh = (N, 8, 16, A)
    other = np.where(rng.random(sh) < 0.5, rng.choice(np.array([1, 2, W - 2]), sh), rng.integers(0, W, sh))
    E = np.where(rng.random(sh) < 0.7, (W - 1) * rng.integers(0, 2, sh), other)
    M = (rng.random(sh) < rng.choice(np.array([0.0, 0.5, 1.0]), (N, 8, 1, A))).astype(np.int64)
    i = np.arange(P) * S; q = N - 1
    for r in (0, q):
        for g in range(8):
            k = 2 * rng.integers(0, 8, P); E[r, g, k, i] = W - 1; M[r, g, k, i] = 1
    E[1, 0, :, 0::S] = 0; M[1, 0, :, 0::S] = 0
    E[q, 0, :, 0] = 0; M[q, 0, :, 0] = 0
    a, b, c, d = int(i[CAP - 1]), int(i[P - 1]), int(i[P - 2]), int(i[3])
    E[q, 7, :, a] = W - 1; M[q, 7, :, a] = 1
    E[q, 7, :, b] = 0; M[q, 7, :, b] = 0; E[q, 7, 14:, b] = W - 1; M[q, 7, 14:, b] = 1
    E[q, 7, :, c] = 0; M[q, 7, :, c] = 0; E[q, 7, 14, c] = W - 2; M[q, 7, 14, c] = 1; E[q, 7, 15, c] = 1
    E[:, 7, 0::2, d] = 2; M[:, 7, 0::2, d] = 1; E[:, 7, 1::2, d] = W - 1; M[:, 7, 1::2, d] = 0
    return pack(X, E, M)
def setup_inputs_corners(rng):
    fat = rng.random((N, 8, W)) < 0.5; X = cols(rng, counts(rng, fat), 255)
    E = lines(rng, fat, 0.1); M = rng.integers(0, 2, (N, 8, 16, A)); g, n = first(X)
    room = (0, 1, CAP - 1, CAP, CAP + 1, P, CAP, P - 1); even = np.arange(16)[:, None] % 2 == 0
    for q in range(N):
        for b in range(8):
            gg = g[q, b]; hot = np.flatnonzero((n[q, b] >= 9) & (gg != 0)); thin = np.flatnonzero(n[q, b] <= 8)
            c = int(rng.choice(np.array(room)))
            if q == 0: c = room[b]
            if q == N - 1: c = room[(b + 4) % 8]
            o = np.concatenate([np.array([P - 1]), rng.permutation(P - 1)]); yes = o[:c]; z = np.zeros((1, P), bool); z[0, o[c:]] = True
            e = np.where(rng.random((16, P)) < 0.2, (W - 1) * rng.integers(0, 2, (16, P)), rng.integers(0, W, (16, P)))
            m = (rng.random((16, P)) < rng.choice(np.array([0.0, 0.5, 1.0]), (1, P))).astype(np.int64)
            ge = gg[e]; m = np.where(even & z & (ge != 0), (ge > 0).astype(np.int64), m)
            e = np.where(~even & z, rng.choice(thin, (16, P)), e)
            k = 2 * rng.integers(0, 8, c); hh = rng.choice(hot, c); e[k, yes] = hh; m[k, yes] = (gg[hh] < 0).astype(np.int64)
            E[q, b, :, 0::S] = e; M[q, b, :, 0::S] = m
    return pack(X, E, M)
def setup_inputs_ties(rng):
    fat = rng.random((N, 8, W)) < 0.5
    n = np.where(fat, np.where(rng.random((N, 8, W)) < 0.8, 9, 16), 8); X = cols(rng, n, rng.choice(np.array([1, 2, 3]), (N, 8, 1, W)))
    E = lines(rng, fat, rng.choice(np.array([0.02, 0.2, 0.5]), (N, 8, 1, A)))
    E = np.take_along_axis(E, rng.integers(0, 3, (N, 8, 16, A)), 2)
    return pack(X, E, (rng.random((N, 8, 16, A)) < rng.choice(np.array([0.1, 0.5, 0.9]), (N, 8, 1, A))).astype(np.int64))
def setup_inputs_deep(rng):
    fat = rng.random((N, 8, W)) < 0.5; X = cols(rng, counts(rng, fat), 255)
    X[..., 0] = 0
    X[..., 3] = 253; X[..., hop(3, 64768 & (W - 1))] = 255
    X[..., 5] = 252; X[..., hop(5, 64512 & (W - 1))] = 255
    X[..., 7] = 255; X[..., hop(7, 65280 & (W - 1))] = 255; X[..., hop(7, 62976 & (W - 1))] = 255
    X[..., 11] = W >> 8
    X[..., W - 3] = top16(W - 21); X[..., hop(W - 3, W - 21)] = 0; X[..., hop(W - 3, W - 21) + 1] = 255
    X[..., 1001] = 255; X[..., 0, 1001] = 254; X[..., hop(1001, 65279 & (W - 1))] = 0
    X[..., 13] = 0; X[..., 7:, 13] = 255; X[..., hop(13, 52785 & (W - 1))] = 0
    X[..., 17] = 0; X[..., :9, 17] = 255; X[..., hop(17, 20655 & (W - 1))] = 0
    E = lines(rng, fat, 0.1); M = rng.integers(0, 2, (N, 8, 16, A)); s, n = first(X)
    h = hop(np.arange(W).reshape(1, 1, W), np.add.reduce(X * WT.reshape(1, 1, 16, 1), axis=2) & (W - 1))
    kind = np.argsort(rng.random((N, 8, P)), axis=-1) % 7
    for q in range(N):
        for b in range(8):
            if b in (1, 6):
                far = np.arange(W) >= (W >> 2); nn = n[q, b]; hh = h[q, b]
                thin = np.flatnonzero((nn <= 8) & far); hot = np.flatnonzero((nn >= 9) & (s[q, b] < 0) & (nn[hh] <= 8) & far[hh])
                E[q, b] = rng.choice(thin, (16, A))
                c = int(rng.integers(CAP >> 3, (CAP >> 2) + 1)); i = S * rng.permutation(P)[:c]; k = 2 * rng.integers(0, 8, c)
                E[q, b, k, i] = rng.choice(hot, c); M[q, b, k, i] = 1
                continue
            for v in range(1, 7):
                i = S * np.flatnonzero(kind[q, b] == v); k = 2 * rng.integers(0, 8, len(i))
                E[q, b, :, i] = 0; M[q, b, :, i] = 0
                if v == 1:
                    for w, e, m in ((0, 3, 1), (2, 3, 1), (4, 3, 1), (6, 5, 1), (7, 7, 1), (8, 7, 0), (9, 7, 1), (10, 7, 0), (11, 7, 1), (12, 7, 0), (13, 7, 0), (14, 7, 0)):
                        E[q, b, w, i] = e; M[q, b, w, i] = m
                elif v == 2:
                    E[q, b, k, i] = W - 3; M[q, b, k, i] = 1
                elif v == 3:
                    E[q, b, k, i] = 11; M[q, b, k, i] = 1; E[q, b, k + 1, i] = 7
                else:
                    E[q, b, k, i] = (1001, 13, 17)[v - 4]; M[q, b, k, i] = 1
    return pack(X, E, M)
def check_inputs(d):
    bad = []
    for k, lo, hi in (("xt", 0, 255), ("led", 0, W - 1), ("mk", 0, 1)):
        v = np.asarray(d[k]).astype(np.float64)
        if np.min(v) < lo or np.max(v) > hi or np.any(v != np.floor(v)): bad.append("range of " + k)
    return bad
def look(X, ix):
    return np.take_along_axis(X, ix.reshape(N, 8, 1, 16 * P), 3).reshape(N, 8, 16, 16, P)
def reference(xt, led, mk):
    X = xt.astype(np.float32).astype(np.int64).reshape(N, 8, 16, W)
    E = led.astype(np.int64).reshape(N, 8, 16, A); M = mk.astype(np.float32).astype(np.int64).reshape(N, 8, 16, A)
    kappa = np.zeros((N, 1, 1, 1), np.int64); ks = np.arange(16).reshape(1, 1, 16, 1)
    for t in range(RO):
        c = t % S; e = E[:, :, :, c::S].copy(); m = M[:, :, :, c::S].copy()
        x = look(X, e); q = x.copy(); b = np.zeros((N, 8, 16, P), np.int64)
        for k in range(16):
            mm = m[:, :, k][:, :, None, :]
            if k % 2 == 0: b = b + mm * x[:, :, :, k]
            else:
                q[:, :, :, k] = np.minimum(b, x[:, :, :, k]); b = b - mm * q[:, :, :, k]
        u = np.add.reduce(WT.reshape(1, 1, 16, 1, 1) * q, axis=2) & (W - 1)
        h = (((e * u) >> 5) + e + kappa) & (W - 1)
        g = np.add.reduce(np.sign(look(X, h) - q), axis=2); over = np.add.reduce((q > 0).astype(np.int64), axis=2)
        con = (over >= 9) & (((m == 1) & (g < 0)) | ((m == 0) & (g > 0)))
        best = np.argmax(np.where(con, np.abs(g), 0), axis=2)
        flip = np.any(con, axis=2)
        win = flip[:, :, None, :] & (ks == best[:, :, None, :])
        E[:, :, :, c::S] = np.where(win, h, e); M[:, :, :, c::S] = np.where(win, 1 - m, m)
        f = flip.astype(np.int64); kappa = (np.add.reduce(f.reshape(N, 8 * P), axis=1) & 31).reshape(N, 1, 1, 1)
        place = np.add.accumulate(f, axis=2) - 1; go = flip & (place < CAP)
        qb = np.take_along_axis(q, best[:, :, None, None, :], 3)[:, :, :, 0]; ub = np.take_along_axis(u, best[:, :, None, :], 2)[:, :, 0]
        new = X.copy()
        for r in range(N):
            d = (r + 1 + t % (N - 1)) % N
            for v in range(8):
                i = np.flatnonzero(go[r, v]); col = BL * place[r, v, i] + (ub[r, v, i] & (BL - 1))
                new[d, v][:, col] = (X[d, v][:, col] + qb[r, v][:, i]) >> 1
        X = new
    return {"yx": X.reshape(N, 128, W).astype(np.float32).astype(BF), "yl": E.reshape(N, 128, A).astype(np.float32), "ym": M.reshape(N, 128, A).astype(np.float32).astype(BF)}

@@ -1,0 +1,645 @@
+import numpy as np
+from concourse.bass import DstId, RemoteDMATransfer
+from concourse.mybir import dt, AluOpType, AxisListType, ActivationFunctionType
+
+ROUNDS = 4
+FUSE, NF, BYV = True, 2, ()
+SW = 288
+TW = 8448
+SCRATCH = {
+    "TB": ("sbuf", [128, TW], "bfloat16"),
+    "LEDI": ("sbuf", [128, 512], "int32"), "MKI": ("sbuf", [128, 512], "bfloat16"), "MS": ("sbuf", [128, 512], "float32"),
+    "CB": ("sbuf", [128, 16, 16, 2], "float32"),
+    "EX": ("sbuf", [128, 16, 32], "float32"), "EY": ("sbuf", [128, 16, 32], "float32"),
+    "LL": ("sbuf", [128, 16, 16], "float32"), "M2": ("sbuf", [128, 256], "float32"),
+    "YLB": ("sbuf", [128, 512], "float32"), "YMB": ("sbuf", [128, 512], "bfloat16"),
+    "Q": ("sbuf", [128, 4096], "bfloat16"), "MX": ("sbuf", [128, 4096], "bfloat16"), "SB": ("sbuf", [128, 4096], "bfloat16"),
+    "D": ("sbuf", [128, 4096], "bfloat16"), "ZB": ("sbuf", [128, 4096], "bfloat16"), "DS": ("sbuf", [128, 4096], "bfloat16"),
+    "MM": ("sbuf", [128, 4096], "bfloat16"),
+    "UI": ("sbuf", [128, 256], "int32"), "UM": ("sbuf", [128, 256], "int32"), "PF": ("sbuf", [128, 256], "float32"),
+    "HI": ("sbuf", [128, 256], "int32"), "HH": ("sbuf", [128, 256], "int32"), "HO": ("sbuf", [128, 256], "uint16"),
+    "UL": ("sbuf", [128, 256], "int32"), "KA": ("sbuf", [128, 256], "float32"), "SGG": ("sbuf", [128, 256], "float32"),
+    "KY": ("sbuf", [128, 256], "float32"), "RM": ("sbuf", [128, 256], "float32"), "MP": ("sbuf", [128, 16], "float32"),
+    "MI": ("sbuf", [128, 16], "int32"), "EB": ("sbuf", [128, 16], "int32"), "FL": ("sbuf", [128, 16], "bfloat16"),
+    "CU": ("sbuf", [128, 16], "bfloat16"), "IX": ("sbuf", [128, 16], "int32"), "IXU": ("sbuf", [128, 16], "uint16"),
+    "S2": ("sbuf", [128, 16], "int32"), "OU": ("sbuf", [128, 16], "uint16"),
+    "SM": ("sbuf", [128, 256], "int32"), "SH": ("sbuf", [128, 256], "int32"),
+    "WN": ("sbuf", [128, 256], "float32"), "W2": ("sbuf", [128, 256], "float32"), "DE": ("sbuf", [128, 256], "float32"),
+    "DW": ("sbuf", [128, 256], "float32"), "OW": ("sbuf", [128, 256], "float32"),
+    "K1": ("sbuf", [128, 8], "int32"), "K2": ("sbuf", [128, 8], "int32"), "K3": ("sbuf", [128, 8], "float32"),
+    "PI": ("sbuf", [128, 8], "int32"), "P4": ("sbuf", [128, 8], "int32"), "P15": ("sbuf", [128, 8], "int32"),
+    "PC": ("sbuf", [128, 8], "int32"), "PF1": ("sbuf", [128, 8], "float32"), "PG": ("sbuf", [128, 8], "float32"),
+    "PR": ("sbuf", [128, 8], "float32"), "PW": ("sbuf", [128, 8], "float32"), "PO": ("sbuf", [128, 8], "float32"),
+    "PE": ("sbuf", [128, 8], "float32"),
+    "IM": ("sbuf", [128, 128], "float32"), "IG": ("sbuf", [128, 128], "float32"), "IR": ("sbuf", [128, 16], "float32"),
+    "IK": ("sbuf", [128, 128], "float32"), "IC": ("sbuf", [128, 16], "int32"),
+    "BD": ("sbuf", [128, 128], "bfloat16"), "IDN": ("sbuf", [128, 128], "bfloat16"), "NID": ("sbuf", [128, 128], "bfloat16"),
+    "I16": ("sbuf", [128, 128], "bfloat16"), "N256": ("sbuf", [128, 128], "bfloat16"), "ONE": ("sbuf", [128, 128], "bfloat16"),
+    "GT": ("sbuf", [128, 128], "bfloat16"), "LT": ("sbuf", [128, 128], "bfloat16"), "LB": ("sbuf", [128, 128], "bfloat16"),
+    "CW": ("sbuf", [128, 144], "bfloat16"), "UW": ("sbuf", [128, 144], "bfloat16"), "RMK": ("sbuf", [128, 16], "float32"),
+    "BR": ("sbuf", [128, 2048], "bfloat16"),
+    "KC": ("sbuf", [128, 256], "float32"), "BS": ("sbuf", [128, 16], "float32"), "FC": ("sbuf", [128, 16], "float32"),
+    "DC": ("sbuf", [128, 128], "bfloat16"), "KD": ("sbuf", [128, 128], "float32"), "CL": ("sbuf", [128, 16], "uint16"),
+    "ZZ": ("sbuf", [128, 16], "bfloat16"),
+    "XP": ("psum", [128, 2048], "float32"), "EP": ("psum", [128, 512], "float32"), "UP": ("psum", [128, 512], "float32"),
+    "ZP": ("psum", [128, 512], "float32"), "SP": ("psum", [128, 512], "float32"),
+}
+for _c in range(2):
+    SCRATCH["OFF%d" % _c] = ("sbuf", [128, 256], "uint16")
+    SCRATCH["E%d" % _c] = ("sbuf", [128, 256], "float32")
+    SCRATCH["SG%d" % _c] = ("sbuf", [128, 256], "float32")
+    SCRATCH["MB%d" % _c] = ("sbuf", [128, 256], "bfloat16")
+for _t in range(ROUNDS):
+    SCRATCH["SN%d" % _t] = ("sbuf", [128, SW], "bfloat16")
+    SCRATCH["LD%d" % _t] = ("sbuf", [128, SW], "bfloat16")
+SEMAPHORES = (["qV", "qS", "qP", "qG", "loc"] + ["d%d" % i for i in range(6)]
+              + ["arr%d" % t for t in range(ROUNDS)] + ["hop%d" % t for t in range(ROUNDS)])
+
+
+def helpers(core, dst, topo):
+    if topo.may_write(core, dst):
+        return []
+    own = [c for c in topo.cores_of(core) if c != core and topo.may_write(c, dst)]
+    near = [c for c in own if topo.die(c) == topo.die(core)]
+    return (near or own)[:2]
+
+
+def target(rank, t, n):
+    return (rank + 1 + t % (n - 1)) % n
+
+
+def emask(engines):
+    m = 0
+    for e in engines:
+        m |= 1 << e
+    return m
+
+
+def parts_of(n):
+    w = SW // n
+    return [(i * w, (i + 1) * w) for i in range(n)]
+
+
+def bridge(g, core, T, topo):
+    n = len(T.cores)
+    sent = 0
+    for t in range(ROUNDS):
+        for r in range(n):
+            src, dst = T.cores[r], T.cores[target(r, t, n)]
+            hs = helpers(src, dst, topo)
+            if core not in hs:
+                continue
+            lo, hi = parts_of(len(hs))[hs.index(core)]
+            k = len(topo.engines(src, core)) // len(hs)
+            g.wait_ge(T.sem["hop%d" % t], k)
+            rid, pid = topo.addr(dst, core)
+            g.remote_dma(T["LD%d" % t][:, lo:hi], T["LD%d" % t][:, lo:hi], T.sem["arr%d" % t], T.sem.loc, pid, rid, topo.mask(core, dst))
+            sent += len(topo.engines(core, dst))
+    if sent:
+        g.wait_ge(T.sem.loc, sent)
+
+
+def rank_program(g, core, T, topo):
+    rank = T.rank_of(core)
+    if rank is None:
+        bridge(g, core, T, topo)
+        return
+    A, F = AluOpType, ActivationFunctionType
+    n = len(T.cores)
+    Qs = {"V": g.vector, "S": g.scalar, "P": g.tensor, "G": g, "Y": g.sync}
+    seq = {"V": 0, "S": 0, "P": 0, "G": 0}
+    known = {q: {} for q in Qs}
+    log = {}
+    masks = {}
+
+    def a(name, *idx):
+        key = (name, str(idx))
+        if key not in masks:
+            shape = SCRATCH[name][1][1:]
+            bits = np.zeros(int(np.prod(shape)), np.uint8)
+            ids = np.arange(bits.size).reshape(shape)
+            bits[(ids[idx] if idx else ids).ravel()] = 1
+            exact = int.from_bytes(np.packbits(bits).tobytes(), "big")
+            bank = exact
+            if SCRATCH[name][0] == "psum":
+                wide = bits.copy()
+                for b in range(0, bits.size, 512):
+                    if bits[b:b + 512].any():
+                        wide[b:b + 512] = 1
+                bank = int.from_bytes(np.packbits(wide).tobytes(), "big")
+            masks[key] = (exact, bank)
+        return (name, T[name][(slice(None),) + tuple(idx)], masks[key][0], masks[key][1])
+
+    def c(name, lo, hi, step=1):
+        return a(name, slice(lo, hi, step) if step != 1 else slice(lo, hi))
+
+    def w(name):
+        return a(name)
+
+    def order(q, reads, writes):
+        need = {}
+        for isw, lst in ((False, reads), (True, writes)):
+            for name, _, ex, bk in lst:
+                psum = SCRATCH[name][0] == "psum"
+                for rq, src, cnt, rw, rex, rbk, clk in log.get(name, []):
+                    if psum and rq != q:
+                        hit = bk & rbk
+                    elif psum and q == "P":
+                        hit = 0
+                    else:
+                        hit = (isw or rw) and (ex & rex)
+                    if hit and need.get(src, (0, None))[0] < cnt:
+                        need[src] = (cnt, clk)
+        for src in sorted(need, key=lambda s: -len(need[s][1])):
+            cnt, clk = need[src]
+            if known[q].get(src, 0) < cnt:
+                Qs[q].wait_ge(T.sem[src], cnt)
+                for s, v in clk.items():
+                    known[q][s] = max(known[q].get(s, 0), v)
+                known[q][src] = max(known[q].get(src, 0), cnt)
+
+    def note(q, src, cnt, reads, writes, clk):
+        for isw, lst in ((False, reads), (True, writes)):
+            for name, _, ex, bk in lst:
+                old = log.get(name, [])
+                if isw:
+                    old = [x for x in old if x[4] & ~ex]
+                old.append((q, src, cnt, isw, ex, bk, clk))
+                log[name] = old
+
+    def run(q, fn, writes, reads):
+        order(q, reads, writes)
+        src = "q" + q
+        fn(Qs[q]).then_inc(T.sem[src], 1)
+        seq[q] += 1
+        clk = dict(known[q])
+        clk[src] = seq[q]
+        note(q, src, seq[q], reads, writes, clk)
+
+    def dma(q, sem, out, in_):
+        reads = [in_] if isinstance(in_, tuple) else []
+        writes = [out] if isinstance(out, tuple) else []
+        order(q, reads, writes)
+        Qs[q].dma_start(out[1] if writes else out, in_[1] if reads else in_).then_inc(T.sem[sem], 16)
+        note(q, sem, 16, reads, writes, dict(known[q]))
+
+    def ind(win, off):
+        return ("ind", win, off)
+
+    def opnd(x, reads):
+        if x[0] == "ind":
+            reads += [x[1], x[2]]
+            return x[1][1].indirect(x[2][1])
+        reads.append(x)
+        return x[1]
+
+    def sc(x, reads):
+        return opnd(x, reads) if isinstance(x, tuple) else x
+
+    def tt(out, in0, in1, op):
+        r = []
+        i0, i1 = opnd(in0, r), opnd(in1, r)
+        run("V", lambda e: e.tensor_tensor(out[1], i0, i1, op), [out], r)
+
+    def ts(out, in0, s1, op0, s2=None, op1=None):
+        r = []
+        i0, x1 = opnd(in0, r), sc(s1, r)
+        if op1 is None:
+            run("V", lambda e: e.tensor_scalar(out[1], i0, x1, None, op0), [out], r)
+        else:
+            x2 = sc(s2, r)
+            run("V", lambda e: e.tensor_scalar(out[1], i0, x1, x2, op0, op1), [out], r)
+
+    def cp(out, in_):
+        r = []
+        i0 = opnd(in_, r)
+        run("V", lambda e: e.tensor_copy(out[1], i0), [out], r)
+
+    def scatter(win, off, in_):
+        run("V", lambda e: e.tensor_copy(win[1].indirect(off[1]), in_[1]), [win], [in_, off])
+
+    def scan(out, d0, d1, op0, op1):
+        run("V", lambda e: e.tensor_tensor_scan(out[1], d0[1], d1[1], 0.0, op0, op1), [out], [d0, d1])
+
+    def fill(out, v):
+        run("V", lambda e: e.memset(out[1], v), [out], [])
+
+    def turn(out, in_):
+        run("V", lambda e: e.transpose(out[1], in_[1]), [out], [in_])
+
+    def act(out, in_, func, scale=None, bias=None):
+        r = []
+        i0 = opnd(in_, r)
+        kw = {}
+        if scale is not None:
+            kw["scale"] = sc(scale, r)
+        if bias is not None:
+            kw["bias"] = sc(bias, r)
+        run("S", lambda e: e.activation(out[1], i0, func, **kw), [out], r)
+
+    def mm(out, lhsT, rhs, start=True, stop=True):
+        run("P", lambda e: e.matmul(out[1], lhsT[1], rhs[1], start, stop), [out], [lhsT, rhs])
+
+    def iota(out, pattern, base, cm, flag=True):
+        if flag:
+            run("G", lambda e: e.iota(out[1], pattern, base, cm, allow_small_or_imprecise_dtypes=True), [out], [])
+        else:
+            run("G", lambda e: e.iota(out[1], pattern, base, cm), [out], [])
+
+    dma("Y", "d0", w("LEDI"), T.led[:])
+    dma("S", "d1", w("MKI"), T.mk[:])
+    dma("Y", "d2", c("TB", 0, 2048), T.xt[:])
+
+    iota(c("PI", 0, 1), [[0, 1]], 0, 1, False)
+    iota(w("IG"), [[1, 8], [0, 16]], 0, 0)
+    iota(w("IR"), [[1, 16]], 0, 0)
+    iota(w("IM"), [[1, 128]], 0, 0)
+    iota(w("DC"), [[0, 64], [-4096, 2]], 4096, 0)
+    iota(w("IK"), [[0, 8], [1, 16]], 0, 0)
+    iota(w("KC"), [[0, 16], [-256, 16]], 3840, 0)
+    iota(w("BS"), [[256, 16]], 240, 0)
+    iota(w("FC"), [[16, 16]], 4096, 0)
+    iota(w("IC"), [[1, 16]], 0, 0, False)
+    iota(c("TB", 2048, TW), [[0, TW - 2048]], 0, 0)
+
+    ts(c("PC", 0, 1), c("PI", 0, 1), 4, A.arith_shift_right, 1, A.bitwise_and)
+    ts(c("P4", 0, 1), c("PI", 0, 1), 4, A.arith_shift_right)
+    ts(c("P15", 0, 1), c("PI", 0, 1), 15, A.bitwise_and)
+    cp(c("PO", 0, 1), c("PC", 0, 1))
+    ts(c("PE", 0, 1), c("PC", 0, 1), -1.0, A.mult, 1.0, A.add)
+    cp(c("PG", 0, 1), c("P4", 0, 1))
+    cp(c("PR", 0, 1), c("P15", 0, 1))
+    cp(c("PF1", 0, 1), c("PI", 0, 1))
+    ts(c("PW", 0, 1), c("P15", 0, 1), 2.0, A.mult, 1.0, A.add)
+    pg, pr, pp, pw = c("PG", 0, 1), c("PR", 0, 1), c("PF1", 0, 1), c("PW", 0, 1)
+    podd, peven = c("PO", 0, 1), c("PE", 0, 1)
+    ts(w("BD"), w("IG"), pg, A.is_equal)
+    ts(w("RMK"), w("IR"), pr, A.is_equal)
+    for r in range(8):
+        ts(c("BR", 128 * r, 128 * r + 128), w("BD"), c("RMK", r, r + 1), A.mult)
+
+    def early_constants():
+        for r in range(8, 16):
+            ts(c("BR", 128 * r, 128 * r + 128), w("BD"), c("RMK", r, r + 1), A.mult)
+        ts(w("IDN"), w("IM"), pp, A.is_equal)
+        fill(w("CW"), 0.0)
+        ts(c("CW", 15, 143, 16), c("IG", 0, 128, 16), pg, A.is_equal)
+        ts(w("UW"), w("CW"), pw, A.mult)
+
+    def scan_constants():
+        for k in range(16):
+            fill(c("MX", 256 * k + 240, 256 * k + 256), 4096.0)
+
+    def late_constants():
+        ts(w("NID"), w("IDN"), -1.0, A.mult)
+        ts(w("I16"), w("IDN"), 16.0, A.mult)
+        ts(w("N256"), w("IDN"), -256.0, A.mult)
+        fill(w("ONE"), 1.0)
+        fill(w("ZZ"), 0.0)
+        ts(w("GT"), w("IM"), pp, A.is_gt)
+        ts(w("KD"), w("IK"), 0.5, A.is_gt)
+        tt(w("LT"), w("GT"), w("BD"), A.mult)
+        tt(w("LB"), w("LT"), w("BD"), A.subtract)
+        ts(w("BS"), w("BS"), pr, A.add)
+        ts(w("FC"), w("FC"), pr, A.add)
+        cp(w("CL"), w("IC"))
+
+    def expand(src3, second):
+        h0, h1 = slice(0, 16), slice(16, 32)
+        ts(a("EX", slice(None), h0), src3, peven, A.mult)
+        if second == "S":
+            act(a("EX", slice(None), h1), src3, F.Copy, scale=podd)
+        else:
+            ts(a("EX", slice(None), h1), src3, podd, A.mult)
+        turn(w("EY"), w("EX"))
+        return a("EY", slice(None), h0), a("EY", slice(None), h1)
+
+    def to_lists(cl):
+        h0, h1 = expand(a("CB", slice(None), slice(None), cl), "V" if cl else "S")
+        tt(w("LL"), h0, h1, A.add)
+        m2 = w("M2")
+        ts(m2, w("LL"), 2047.5, A.is_ge, -2048.0, A.mult)
+        tt(w("E%d" % cl), w("LL"), m2, A.add)
+        ts(w("MB%d" % cl), m2, -255.0 / 2048.0, A.mult)
+        cp(w("OFF%d" % cl), w("E%d" % cl))
+        ts(w("SG%d" % cl), m2, 8.0, A.mult, 8192.0, A.add)
+
+    def masks_of(cl, pairs, by_v):
+        for i in pairs:
+            o = 512 * (i % 4)
+            for k in (0, 1):
+                mm(c("XP", o + 256 * k, o + 256 * k + 256), c("BR", 128 * (2 * i + k), 128 * (2 * i + k) + 128), w("MB%d" % cl))
+            for k in (0, 1):
+                out, src = c("MM", 2 * i + k, 4096, 16), c("XP", o + 256 * k, o + 256 * k + 256)
+                if i in by_v:
+                    cp(out, src)
+                else:
+                    act(out, src, F.Copy)
+
+    def lines_to_psum(cl, first):
+        e = w("E%d" % cl)
+        act(c("EP", 0, 256), e, F.Copy)
+        if first:
+            act(c("EP", 256, 512), e, F.Copy, scale=32.0)
+        else:
+            act(c("EP", 256, 512), e, F.Identity, scale=32.0, bias=c("K3", 0, 1))
+
+    def items():
+        return c("TB", 0, 2048)
+
+    def quarter(name, q):
+        return c(name, 1024 * q, 1024 * q + 1024)
+
+    def lists(name, q):
+        return c(name, 64 * q, 64 * q + 64)
+
+    def gather_x(cl, q, eng):
+        src = ind(items(), lists("OFF%d" % cl, q))
+        if eng == "S":
+            act(quarter("Q", q), src, F.Copy)
+        else:
+            cp(quarter("Q", q), src)
+
+    def lift(q):
+        for b in (2 * q, 2 * q + 1):
+            o = 512 * (b % 4)
+            mm(c("XP", o, o + 512), w("IDN"), c("Q", 512 * b, 512 * b + 512))
+
+    def marked_gather(cl, q):
+        tt(quarter("MX", q), ind(items(), lists("OFF%d" % cl, q)), quarter("MM", q), A.min)
+        for k in range(4 * q, 4 * q + 4):
+            fill(c("MX", 256 * k + 240, 256 * k + 256), 4096.0)
+
+    def marked(q):
+        for k in range(4 * q, 4 * q + 4):
+            o = 256 * (k % 8)
+            tt(c("MX", 256 * k, 256 * k + 240), c("XP", o, o + 240), c("MM", 256 * k, 256 * k + 240), A.min)
+
+    def balances(h):
+        for r in range(16):
+            lo, hi = 2048 * h + r, 2048 * h + 2048
+            scan(c("SB", lo, hi, 16), c("MX", lo, hi, 16), w("DC"), A.subtract, A.min)
+
+    def odd_amounts(h):
+        for r in range(16):
+            lo, hi = 2048 * h + r, 2048 * h + 2048
+            tt(c("Q", lo + 16, hi, 32), c("XP", 16 + r, 2048, 32), c("SB", lo, hi, 32), A.min)
+
+    def sum_u(h, odd):
+        for r in range(16):
+            lo, hi = 2048 * h + r + 16 * odd, 2048 * h + 2048
+            mm(c("UP", 128 * h + odd, 128 * h + 128, 2), c("UW", 15 - r, 143 - r), c("Q", lo, hi, 32), r == 0, r == 15)
+
+    def count_over(q):
+        for r in range(16):
+            mm(lists("ZP", q), c("CW", 15 - r, 143 - r), c("ZB", 1024 * q + r, 1024 * q + 1024, 16), r == 0, r == 15)
+
+    def score(q):
+        o = 64 * q if q < 2 else 320 + 64 * (q - 2)
+        for r in range(16):
+            mm(c("SP" if q < 2 else "UP", o, o + 64), c("CW", 15 - r, 143 - r), c("DS", 1024 * q + r, 1024 * q + 1024, 16), r == 0, r == 15)
+
+    def hashes(h):
+        s = (128 * h, 128 * h + 128)
+        cp(c("UI", *s), c("UP", *s))
+        ts(c("UM", *s), c("UI", *s), 2047, A.bitwise_and)
+        tt(c("PF", *s), c("UM", *s), c("EP", *s), A.mult)
+        tt(c("HI", *s), c("PF", *s), c("EP", 256 + s[0], 256 + s[1]), A.add)
+        ts(c("HH", *s), c("HI", *s), 5, A.arith_shift_right, 2047, A.bitwise_and)
+        cp(c("HO", *s), c("HH", *s))
+
+    def low_keys(h):
+        s = (128 * h, 128 * h + 128)
+        ts(c("UL", *s), c("UM", *s), 15, A.bitwise_and)
+        tt(c("KA", *s), c("UL", *s), c("KC", *s), A.add)
+
+    def over(q, eng):
+        if eng == "S":
+            act(quarter("ZB", q), quarter("Q", q), F.Sign)
+        else:
+            ts(quarter("ZB", q), quarter("Q", q), 1.0, A.min)
+
+    def gate(cl, lo, hi):
+        ts(c("ZP", lo, hi), c("ZP", lo, hi), 8.5, A.is_ge)
+        tt(c("SGG", lo, hi), c("ZP", lo, hi), c("SG%d" % cl, lo, hi), A.mult)
+
+    def far(q):
+        act(quarter("D", q), ind(items(), lists("HO", q)), F.Copy)
+
+    def minus(b, out):
+        mm(out, w("IDN"), c("D", 512 * b, 512 * b + 512), True, False)
+        mm(out, w("NID"), c("Q", 512 * b, 512 * b + 512), False, True)
+
+    def sign_psum(b, src):
+        act(c("DS", 512 * b, 512 * b + 512), src, F.Sign)
+
+    def diff(q):
+        tt(quarter("D", q), ind(items(), lists("HO", q)), quarter("Q", q), A.subtract)
+
+    def sign(q, eng):
+        if eng == "S":
+            act(quarter("DS", q), quarter("D", q), F.Sign)
+        else:
+            ts(quarter("DS", q), quarter("D", q), 1.0, A.min, -1.0, A.max)
+
+    def keys(h):
+        s = (128 * h, 128 * h + 128)
+        p = c("UP", 320, 448) if h else c("SP", 0, 128)
+        tt(p, p, c("SGG", *s), A.mult)
+        tt(c("KY", *s), p, c("KA", *s), A.add)
+        scan(c("RM", *s), w("KD"), c("KY", *s), A.mult, A.max)
+
+    def send(t):
+        dst = T.cores[target(rank, t, n)]
+        hs = helpers(core, dst, topo)
+        sn = w("SN%d" % t)
+        order("G", [sn], [])
+        if not hs:
+            rid, pid = topo.addr(dst, core)
+            g.remote_dma(T["LD%d" % t][:], sn[1], T.sem["arr%d" % t], T.sem.loc, pid, rid, topo.mask(core, dst))
+            return len(topo.engines(core, dst))
+        tr, cnt = [], 0
+        for i, (lo, hi) in enumerate(parts_of(len(hs))):
+            es = topo.engines(core, hs[i])
+            k = len(es) // len(hs)
+            rid, pid = topo.addr(hs[i], core)
+            tr.append(RemoteDMATransfer(dst_ids=[DstId(rid=rid, pnc=pid)], dma_engine_mask=emask(es[i * k:(i + 1) * k]),
+                                        remote_sem=T.sem["hop%d" % t], srcs=[T["SN%d" % t][:, lo:hi]], dsts=[T["LD%d" % t][:, lo:hi]]))
+            cnt += k
+        g.remote_dma_fused(tr, local_sem=T.sem.loc)
+        return cnt
+
+    def arrivals_of(t):
+        src = [r for r in range(n) if target(r, t, n) == rank][0]
+        hs = helpers(T.cores[src], core, topo)
+        cnt = sum(len(topo.engines(h, core)) for h in (hs or [T.cores[src]]))
+        note("R", "arr%d" % t, cnt, [], [w("LD%d" % t)], {})
+
+    def winners(t):
+        tt(w("MP"), c("RM", 15, 256, 16), w("FC"), A.max)
+        cp(w("MI"), w("MP"))
+        ts(w("FL"), w("MP"), 8191.5, A.is_ge)
+        ts(w("EB"), w("MI"), 4, A.arith_shift_right, 240, A.bitwise_and)
+        scan(w("CU"), w("FL"), w("ZZ"), A.add, A.max)
+        tt(w("IX"), w("BS"), w("EB"), A.subtract)
+        ts(w("S2"), w("MI"), 255, A.bitwise_and)
+        cp(w("IXU"), w("IX"))
+        pl = c("UP", 256, 272)
+        mm(pl, w("LB"), w("FL"), True, False)
+        mm(pl, w("N256"), w("FL"), False, False)
+        mm(pl, w("BD"), w("CU"), False, True)
+        cp(c("SN%d" % t, 272, 288), w("S2"))
+        cp(c("SN%d" % t, 0, 256), ind(w("Q"), w("IXU")))
+        act(c("SN%d" % t, 256, 272), pl, F.Copy)
+
+    def kappa():
+        mm(c("UP", 288, 289), w("ONE"), c("CU", 15, 16))
+        ts(c("K1", 0, 1), c("UP", 288, 289), 32.0, A.mult)
+        ts(c("K2", 0, 1), c("K1", 0, 1), 1023, A.bitwise_and)
+        cp(c("K3", 0, 1), c("K2", 0, 1))
+
+    def flipped():
+        tt(w("WN"), ind(w("MP"), w("CL")), w("KY"), A.is_equal)
+
+    def moves(cl):
+        tt(w("DE"), w("HH"), c("EP", 0, 256), A.subtract)
+
+    def flips(cl):
+        e = w("E%d" % cl)
+        flipped()
+        tt(w("DW"), w("DE"), w("WN"), A.mult)
+        ts(w("W2"), w("WN"), -2.0, A.mult, 1.0, A.add)
+        tt(e, e, w("DW"), A.add)
+        tt(w("SG%d" % cl), w("SG%d" % cl), w("W2"), A.mult)
+
+    def renew(cl):
+        cp(w("OFF%d" % cl), w("E%d" % cl))
+        ts(w("MB%d" % cl), w("SG%d" % cl), -255.0 / 8192.0, A.mult, 0.0, A.max)
+
+    def last(cl):
+        ts(w("DW"), w("SG%d" % cl), -0.125, A.mult, 1024.0, A.add)
+        tt(w("LL"), w("DW"), w("E%d" % cl), A.add)
+        h0, h1 = expand(w("LL"), "V")
+        tt(w("OW"), h0, h1, A.add)
+
+    def out_columns(cl):
+        m2 = w("M2")
+        ts(m2, w("OW"), 2047.5, A.is_ge, -2048.0, A.mult)
+        act(c("YMB", cl, 512, 2), m2, F.Copy, scale=-1.0 / 2048.0)
+        tt(c("YLB", cl, 512, 2), w("OW"), m2, A.add)
+
+    def apply(t):
+        arrivals_of(t)
+        ld = "LD%d" % t
+        of = c("UP", 272, 288)
+        mm(of, w("I16"), c(ld, 256, 272), True, False)
+        mm(of, w("IDN"), c(ld, 272, 288), False, True)
+        ts(w("OU"), of, 4096.0, A.add)
+        tt(w("SM"), ind(w("TB"), w("OU")), c(ld, 0, 256), A.add)
+        ts(w("SH"), w("SM"), 1, A.arith_shift_right)
+        scatter(w("TB"), w("OU"), w("SH"))
+
+    act(w("MS"), w("MKI"), F.Copy, scale=2048.0)
+    tt(w("CB"), w("LEDI"), w("MS"), A.add)
+    to_lists(0)
+    early_constants()
+    gather_x(0, 0, "S")
+    masks_of(0, range(8), (0, 1, 2, 3, 4, 6))
+    lines_to_psum(0, True)
+    scan_constants()
+    total = 0
+    for t in range(ROUNDS):
+        cl, nx = t % 2, 1 - t % 2
+        bank = [c("XP", 512 * b, 512 * b + 512) for b in range(4)]
+        if t:
+            gather_x(cl, 0, "S")
+        if FUSE:
+            gather_x(cl, 1, "S")
+            marked_gather(cl, 1)
+        else:
+            gather_x(cl, 1, "V")
+        gather_x(cl, 2, "S")
+        gather_x(cl, 3, "S")
+        lift(0)
+        lift(1)
+        marked(0)
+        if not FUSE:
+            marked(1)
+        sum_u(0, 0)
+        balances(0)
+        odd_amounts(0)
+        lift(2)
+        sum_u(0, 1)
+        over(0, "V")
+        over(1, "S")
+        marked(2)
+        lift(3)
+        hashes(0)
+        marked(3)
+        count_over(0)
+        count_over(1)
+        sum_u(1, 0)
+        for q in range(NF):
+            far(q)
+        balances(1)
+        odd_amounts(1)
+        sum_u(1, 1)
+        low_keys(0)
+        if t == 0:
+            late_constants()
+            to_lists(1)
+        for b in range(2 * NF):
+            minus(b, bank[b])
+        over(2, "S")
+        if NF < 2:
+            diff(1)
+        hashes(1)
+        for b in range(2):
+            sign_psum(b, bank[b])
+        over(3, "S")
+        if NF == 2:
+            for b in range(2, 4):
+                sign_psum(b, bank[b])
+        else:
+            sign(1, "S")
+        diff(2)
+        count_over(2)
+        score(0)
+        count_over(3)
+        score(1)
+        sign(2, "S")
+        diff(3)
+        sign(3, "V")
+        low_keys(1)
+        gate(cl, 0, 256)
+        score(2)
+        keys(0)
+        score(3)
+        moves(cl)
+        if t + 1 == ROUNDS:
+            out_columns(nx)
+        keys(1)
+        winners(t)
+        total += send(t)
+        if t + 1 < ROUNDS:
+            kappa()
+            masks_of(nx, range(8), BYV)
+        flips(cl)
+        if t + 2 < ROUNDS:
+            renew(cl)
+        else:
+            last(cl)
+        if t + 1 < ROUNDS:
+            lines_to_psum(nx, False)
+        apply(t)
+    dma("Y", "d5", T.yx[:], items())
+    out_columns(cl)
+    dma("S", "d3", T.ym[:], w("YMB"))
+    dma("S", "d4", T.yl[:], w("YLB"))
+    for d in ("d3", "d4", "d5"):
+        g.sync.wait_ge(T.sem[d], 16)
+    g.wait_ge(T.sem.loc, total)
+    for q in ("V", "S", "P", "G"):
+        g.wait_ge(T.sem["q" + q], seq[q])
+    for d in ("d0", "d1", "d2"):
+        g.wait_ge(T.sem[d], 16)

@@ -3,13 +3,13 @@ from concourse.bass import DstId, RemoteDMATransfer
 from concourse.mybir import dt, AluOpType, AxisListType, ActivationFunctionType
 
 ROUNDS = 4
-FUSE, NF, BYV = True, 2, ()
+PRE = 4
 SW = 288
 TW = 8448
 SCRATCH = {
     "TB": ("sbuf", [128, TW], "bfloat16"),
-    "LEDI": ("sbuf", [128, 512], "int32"), "MKI": ("sbuf", [128, 512], "bfloat16"), "MS": ("sbuf", [128, 512], "float32"),
-    "CB": ("sbuf", [128, 16, 16, 2], "float32"),
+    "LEDI": ("sbuf", [128, 16, 16, 2], "int32"), "MKI": ("sbuf", [128, 16, 16, 2], "bfloat16"),
+    "MS0": ("sbuf", [128, 16, 16], "float32"), "MS1": ("sbuf", [128, 16, 16], "float32"), "CB": ("sbuf", [128, 16, 16], "float32"), "OFFM": ("sbuf", [128, 256], "uint16"),
     "EX": ("sbuf", [128, 16, 32], "float32"), "EY": ("sbuf", [128, 16, 32], "float32"),
     "LL": ("sbuf", [128, 16, 16], "float32"), "M2": ("sbuf", [128, 256], "float32"),
     "YLB": ("sbuf", [128, 512], "float32"), "YMB": ("sbuf", [128, 512], "bfloat16"),
@@ -248,7 +248,7 @@ def rank_program(g, core, T, topo):
 
     dma("Y", "d0", w("LEDI"), T.led[:])
     dma("S", "d1", w("MKI"), T.mk[:])
-    dma("Y", "d2", c("TB", 0, 2048), T.xt[:])
+    dma("Y", "d2", c("TB", 16, 2064), T.xt[:])
 
     iota(c("PI", 0, 1), [[0, 1]], 0, 1, False)
     iota(w("IG"), [[1, 8], [0, 16]], 0, 0)
@@ -260,7 +260,7 @@ def rank_program(g, core, T, topo):
     iota(w("BS"), [[256, 16]], 240, 0)
     iota(w("FC"), [[16, 16]], 4096, 0)
     iota(w("IC"), [[1, 16]], 0, 0, False)
-    iota(c("TB", 2048, TW), [[0, TW - 2048]], 0, 0)
+    iota(c("TB", 2064, TW), [[0, TW - 2064]], 0, 0)
 
     ts(c("PC", 0, 1), c("PI", 0, 1), 4, A.arith_shift_right, 1, A.bitwise_and)
     ts(c("P4", 0, 1), c("PI", 0, 1), 4, A.arith_shift_right)
@@ -275,27 +275,28 @@ def rank_program(g, core, T, topo):
     podd, peven = c("PO", 0, 1), c("PE", 0, 1)
     ts(w("BD"), w("IG"), pg, A.is_equal)
     ts(w("RMK"), w("IR"), pr, A.is_equal)
-    for r in range(8):
-        ts(c("BR", 128 * r, 128 * r + 128), w("BD"), c("RMK", r, r + 1), A.mult)
 
-    def early_constants():
-        for r in range(8, 16):
-            ts(c("BR", 128 * r, 128 * r + 128), w("BD"), c("RMK", r, r + 1), A.mult)
-        ts(w("IDN"), w("IM"), pp, A.is_equal)
-        fill(w("CW"), 0.0)
-        ts(c("CW", 15, 143, 16), c("IG", 0, 128, 16), pg, A.is_equal)
-        ts(w("UW"), w("CW"), pw, A.mult)
+    def row_masks(lo, hi):
+        for r in range(lo, hi):
+            act(c("BR", 128 * r, 128 * r + 128), w("BD"), F.Copy, scale=c("RMK", r, r + 1))
 
-    def scan_constants():
-        for k in range(16):
-            fill(c("MX", 256 * k + 240, 256 * k + 256), 4096.0)
+    row_masks(0, 8)
+    fill(c("TB", 0, 8), 0.0)
+    fill(c("TB", 8, 16), 4096.0)
+    ts(w("IDN"), w("IM"), pp, A.is_equal)
+    fill(w("CW"), 0.0)
+    ts(c("CW", 15, 143, 16), c("IG", 0, 128, 16), pg, A.is_equal)
+    ts(w("UW"), w("CW"), pw, A.mult)
+
+    ts(w("NID"), w("IDN"), -1.0, A.mult)
+    ts(w("I16"), w("IDN"), 16.0, A.mult)
+    fill(w("ONE"), 1.0)
+    fill(w("ZZ"), 0.0)
+    for k in range(2):
+        act(w("MS%d" % k), a("MKI", slice(None), slice(None), k), F.Copy, scale=4096.0)
 
     def late_constants():
-        ts(w("NID"), w("IDN"), -1.0, A.mult)
-        ts(w("I16"), w("IDN"), 16.0, A.mult)
         ts(w("N256"), w("IDN"), -256.0, A.mult)
-        fill(w("ONE"), 1.0)
-        fill(w("ZZ"), 0.0)
         ts(w("GT"), w("IM"), pp, A.is_gt)
         ts(w("KD"), w("IK"), 0.5, A.is_gt)
         tt(w("LT"), w("GT"), w("BD"), A.mult)
@@ -304,37 +305,45 @@ def rank_program(g, core, T, topo):
         ts(w("FC"), w("FC"), pr, A.add)
         cp(w("CL"), w("IC"))
 
-    def expand(src3, second):
+    def expand(src3, second, first="V"):
         h0, h1 = slice(0, 16), slice(16, 32)
-        ts(a("EX", slice(None), h0), src3, peven, A.mult)
-        if second == "S":
-            act(a("EX", slice(None), h1), src3, F.Copy, scale=podd)
-        else:
-            ts(a("EX", slice(None), h1), src3, podd, A.mult)
+        for h, eng, col in ((h0, first, peven), (h1, second, podd)):
+            if eng == "S":
+                act(a("EX", slice(None), h), src3, F.Copy, scale=col)
+            else:
+                ts(a("EX", slice(None), h), src3, col, A.mult)
+
+    def turned():
         turn(w("EY"), w("EX"))
-        return a("EY", slice(None), h0), a("EY", slice(None), h1)
+        return a("EY", slice(None), slice(0, 16)), a("EY", slice(None), slice(16, 32))
 
-    def to_lists(cl):
-        h0, h1 = expand(a("CB", slice(None), slice(None), cl), "V" if cl else "S")
+    def lines_of(cl):
+        every = slice(None)
+        tt(w("CB"), a("LEDI", every, every, cl), w("MS%d" % cl), A.add)
+        return w("CB")
+
+    def lists_turned(cl):
+        h0, h1 = turned()
         tt(w("LL"), h0, h1, A.add)
-        m2 = w("M2")
-        ts(m2, w("LL"), 2047.5, A.is_ge, -2048.0, A.mult)
-        tt(w("E%d" % cl), w("LL"), m2, A.add)
-        ts(w("MB%d" % cl), m2, -255.0 / 2048.0, A.mult)
-        cp(w("OFF%d" % cl), w("E%d" % cl))
-        ts(w("SG%d" % cl), m2, 8.0, A.mult, 8192.0, A.add)
+        if cl == 0:
+            ts(w("OFFM"), w("LL"), -4080.0, A.add)
+            fill(c("OFFM", 15, 256, 16), 8)
+        ts(w("M2"), w("LL"), 4095.5, A.is_ge, -4096.0, A.mult)
 
-    def masks_of(cl, pairs, by_v):
+    def take_lines(cl):
+        tt(w("E%d" % cl), w("LL"), w("M2"), A.add)
+        cp(w("OFF%d" % cl), w("E%d" % cl))
+
+    def take_marks(cl):
+        ts(w("SG%d" % cl), w("M2"), 4.0, A.mult, 8192.0, A.add)
+
+    def masks_of(cl, pairs):
         for i in pairs:
             o = 512 * (i % 4)
             for k in (0, 1):
                 mm(c("XP", o + 256 * k, o + 256 * k + 256), c("BR", 128 * (2 * i + k), 128 * (2 * i + k) + 128), w("MB%d" % cl))
             for k in (0, 1):
-                out, src = c("MM", 2 * i + k, 4096, 16), c("XP", o + 256 * k, o + 256 * k + 256)
-                if i in by_v:
-                    cp(out, src)
-                else:
-                    act(out, src, F.Copy)
+                act(c("MM", 2 * i + k, 4096, 16), c("XP", o + 256 * k, o + 256 * k + 256), F.Copy)
 
     def lines_to_psum(cl, first):
         e = w("E%d" % cl)
@@ -345,7 +354,7 @@ def rank_program(g, core, T, topo):
             act(c("EP", 256, 512), e, F.Identity, scale=32.0, bias=c("K3", 0, 1))
 
     def items():
-        return c("TB", 0, 2048)
+        return c("TB", 16, 2064)
 
     def quarter(name, q):
         return c(name, 1024 * q, 1024 * q + 1024)
@@ -359,6 +368,13 @@ def rank_program(g, core, T, topo):
             act(quarter("Q", q), src, F.Copy)
         else:
             cp(quarter("Q", q), src)
+
+    def gather_mx(q, eng):
+        src = ind(c("TB", 0, 2064), lists("OFFM", q))
+        if eng == "S":
+            act(quarter("MX", q), src, F.Copy)
+        else:
+            cp(quarter("MX", q), src)
 
     def lift(q):
         for b in (2 * q, 2 * q + 1):
@@ -501,25 +517,26 @@ def rank_program(g, core, T, topo):
     def flipped():
         tt(w("WN"), ind(w("MP"), w("CL")), w("KY"), A.is_equal)
 
-    def moves(cl):
-        tt(w("DE"), w("HH"), c("EP", 0, 256), A.subtract)
+    def moves():
+        tt(c("EP", 256, 512), w("HH"), c("EP", 0, 256), A.subtract)
 
     def flips(cl):
         e = w("E%d" % cl)
         flipped()
-        tt(w("DW"), w("DE"), w("WN"), A.mult)
-        ts(w("W2"), w("WN"), -2.0, A.mult, 1.0, A.add)
-        tt(e, e, w("DW"), A.add)
-        tt(w("SG%d" % cl), w("SG%d" % cl), w("W2"), A.mult)
+        act(c("ZP", 0, 256), w("WN"), F.Copy, scale=-2.0, bias=1.0)
+        tt(w("DW"), c("EP", 256, 512), w("WN"), A.mult)
+        tt(e, c("EP", 0, 256), w("DW"), A.add)
+        tt(w("SG%d" % cl), c("ZP", 0, 256), w("SG%d" % cl), A.mult)
 
     def renew(cl):
         cp(w("OFF%d" % cl), w("E%d" % cl))
-        ts(w("MB%d" % cl), w("SG%d" % cl), -255.0 / 8192.0, A.mult, 0.0, A.max)
+        act(w("MB%d" % cl), w("SG%d" % cl), F.Relu, scale=-255.0 / 8192.0)
 
     def last(cl):
         ts(w("DW"), w("SG%d" % cl), -0.125, A.mult, 1024.0, A.add)
         tt(w("LL"), w("DW"), w("E%d" % cl), A.add)
-        h0, h1 = expand(w("LL"), "V")
+        expand(w("LL"), "V")
+        h0, h1 = turned()
         tt(w("OW"), h0, h1, A.add)
 
     def out_columns(cl):
@@ -535,73 +552,87 @@ def rank_program(g, core, T, topo):
         mm(of, w("I16"), c(ld, 256, 272), True, False)
         mm(of, w("IDN"), c(ld, 272, 288), False, True)
         ts(w("OU"), of, 4096.0, A.add)
-        tt(w("SM"), ind(w("TB"), w("OU")), c(ld, 0, 256), A.add)
+        tt(w("SM"), ind(c("TB", 16, TW), w("OU")), c(ld, 0, 256), A.add)
         ts(w("SH"), w("SM"), 1, A.arith_shift_right)
-        scatter(w("TB"), w("OU"), w("SH"))
+        scatter(c("TB", 16, TW), w("OU"), w("SH"))
 
-    act(w("MS"), w("MKI"), F.Copy, scale=2048.0)
-    tt(w("CB"), w("LEDI"), w("MS"), A.add)
-    to_lists(0)
-    early_constants()
-    gather_x(0, 0, "S")
-    masks_of(0, range(8), (0, 1, 2, 3, 4, 6))
-    lines_to_psum(0, True)
-    scan_constants()
-    total = 0
-    for t in range(ROUNDS):
-        cl, nx = t % 2, 1 - t % 2
-        bank = [c("XP", 512 * b, 512 * b + 512) for b in range(4)]
-        if t:
-            gather_x(cl, 0, "S")
-        if FUSE:
-            gather_x(cl, 1, "S")
-            marked_gather(cl, 1)
-        else:
-            gather_x(cl, 1, "V")
+    def first_half(cl):
+        gather_x(cl, 0, "S")
+        gather_x(cl, 1, "S")
+        marked_gather(cl, 1)
         gather_x(cl, 2, "S")
         gather_x(cl, 3, "S")
         lift(0)
         lift(1)
         marked(0)
-        if not FUSE:
-            marked(1)
         sum_u(0, 0)
         balances(0)
         odd_amounts(0)
+
+    def first_half_0():
+        gather_mx(0, "S")
+        take_lines(0)
+        gather_mx(1, "V")
+        gather_x(0, 0, "S")
+        balances(0)
+        gather_mx(2, "S")
+        gather_x(0, 1, "V")
+        gather_x(0, 2, "S")
+        lift(0)
+        lift(1)
+        take_marks(0)
+        lines_of(1)
+        late_constants()
+        sum_u(0, 0)
+        gather_x(0, 3, "S")
+        lines_to_psum(0, True)
+        odd_amounts(0)
+        gather_mx(3, "V")
+
+    expand(lines_of(0), "S")
+    lists_turned(0)
+    total = 0
+    for t in range(ROUNDS):
+        cl, nx = t % 2, 1 - t % 2
+        bank = [c("XP", 512 * b, 512 * b + 512) for b in range(4)]
+        if t:
+            first_half(cl)
+        else:
+            first_half_0()
         lift(2)
         sum_u(0, 1)
         over(0, "V")
         over(1, "S")
-        marked(2)
+        if t:
+            marked(2)
+        else:
+            expand(w("CB"), "S", "S")
+            row_masks(8, 16)
         lift(3)
         hashes(0)
-        marked(3)
+        if t:
+            marked(3)
         count_over(0)
         count_over(1)
         sum_u(1, 0)
-        for q in range(NF):
-            far(q)
+        far(0)
+        far(1)
         balances(1)
         odd_amounts(1)
         sum_u(1, 1)
         low_keys(0)
-        if t == 0:
-            late_constants()
-            to_lists(1)
-        for b in range(2 * NF):
+        for b in range(4):
             minus(b, bank[b])
         over(2, "S")
-        if NF < 2:
-            diff(1)
         hashes(1)
         for b in range(2):
             sign_psum(b, bank[b])
         over(3, "S")
-        if NF == 2:
-            for b in range(2, 4):
-                sign_psum(b, bank[b])
-        else:
-            sign(1, "S")
+        for b in range(2, 4):
+            sign_psum(b, bank[b])
+        if t == 0:
+            lists_turned(1)
+            ts(w("MB1"), w("M2"), -255.0 / 4096.0, A.mult)
         diff(2)
         count_over(2)
         score(0)
@@ -615,7 +646,9 @@ def rank_program(g, core, T, topo):
         score(2)
         keys(0)
         score(3)
-        moves(cl)
+        if t + 1 < ROUNDS:
+            masks_of(nx, range(PRE))
+        moves()
         if t + 1 == ROUNDS:
             out_columns(nx)
         keys(1)
@@ -623,8 +656,12 @@ def rank_program(g, core, T, topo):
         total += send(t)
         if t + 1 < ROUNDS:
             kappa()
-            masks_of(nx, range(8), BYV)
+        if t == 0:
+            take_lines(1)
+            take_marks(1)
         flips(cl)
+        if t + 1 < ROUNDS:
+            masks_of(nx, range(PRE, 8))
         if t + 2 < ROUNDS:
             renew(cl)
         else:

@@ -3,13 +3,14 @@ from concourse.bass import DstId, RemoteDMATransfer
 from concourse.mybir import dt, AluOpType, AxisListType, ActivationFunctionType
 
 ROUNDS = 4
-PRE = 4
+PRE = 2
 SW = 288
 TW = 8448
 SCRATCH = {
     "TB": ("sbuf", [128, TW], "bfloat16"),
     "LEDI": ("sbuf", [128, 16, 16, 2], "int32"), "MKI": ("sbuf", [128, 16, 16, 2], "bfloat16"),
-    "MS0": ("sbuf", [128, 16, 16], "float32"), "MS1": ("sbuf", [128, 16, 16], "float32"), "CB": ("sbuf", [128, 16, 16], "float32"), "OFFM": ("sbuf", [128, 256], "uint16"),
+    "MS0": ("sbuf", [128, 16, 16], "float32"), "CB": ("sbuf", [128, 16, 16], "float32"), "OFFM": ("sbuf", [128, 256], "uint16"),
+    "OFFX": ("sbuf", [128, 64], "uint16"),
     "EX": ("sbuf", [128, 16, 32], "float32"), "EY": ("sbuf", [128, 16, 32], "float32"),
     "LL": ("sbuf", [128, 16, 16], "float32"), "M2": ("sbuf", [128, 256], "float32"),
     "YLB": ("sbuf", [128, 512], "float32"), "YMB": ("sbuf", [128, 512], "bfloat16"),
@@ -18,8 +19,8 @@ SCRATCH = {
     "MM": ("sbuf", [128, 4096], "bfloat16"),
     "UI": ("sbuf", [128, 256], "int32"), "UM": ("sbuf", [128, 256], "int32"), "PF": ("sbuf", [128, 256], "float32"),
     "HI": ("sbuf", [128, 256], "int32"), "HH": ("sbuf", [128, 256], "int32"), "HO": ("sbuf", [128, 256], "uint16"),
-    "UL": ("sbuf", [128, 256], "int32"), "KA": ("sbuf", [128, 256], "float32"), "SGG": ("sbuf", [128, 256], "float32"),
-    "KY": ("sbuf", [128, 256], "float32"), "RM": ("sbuf", [128, 256], "float32"), "MP": ("sbuf", [128, 16], "float32"),
+    "UL": ("sbuf", [128, 256], "int32"), "KA": ("sbuf", [128, 256], "float32"), "GG": ("sbuf", [128, 256], "float32"),
+    "KY": ("sbuf", [128, 256], "float32"), "RM": ("sbuf", [128, 256], "float32"),
     "MI": ("sbuf", [128, 16], "int32"), "EB": ("sbuf", [128, 16], "int32"), "FL": ("sbuf", [128, 16], "bfloat16"),
     "CU": ("sbuf", [128, 16], "bfloat16"), "IX": ("sbuf", [128, 16], "int32"), "IXU": ("sbuf", [128, 16], "uint16"),
     "S2": ("sbuf", [128, 16], "int32"), "OU": ("sbuf", [128, 16], "uint16"),
@@ -32,14 +33,15 @@ SCRATCH = {
     "PR": ("sbuf", [128, 8], "float32"), "PW": ("sbuf", [128, 8], "float32"), "PO": ("sbuf", [128, 8], "float32"),
     "PE": ("sbuf", [128, 8], "float32"),
     "IM": ("sbuf", [128, 128], "float32"), "IG": ("sbuf", [128, 128], "float32"), "IR": ("sbuf", [128, 16], "float32"),
-    "IK": ("sbuf", [128, 128], "float32"), "IC": ("sbuf", [128, 16], "int32"),
+    "IC": ("sbuf", [128, 16], "int32"), "NBD": ("sbuf", [128, 128], "bfloat16"),
+    "EXM": ("sbuf", [128, 16, 32], "bfloat16"), "EYM": ("sbuf", [128, 16, 32], "bfloat16"),
     "BD": ("sbuf", [128, 128], "bfloat16"), "IDN": ("sbuf", [128, 128], "bfloat16"), "NID": ("sbuf", [128, 128], "bfloat16"),
     "I16": ("sbuf", [128, 128], "bfloat16"), "N256": ("sbuf", [128, 128], "bfloat16"), "ONE": ("sbuf", [128, 128], "bfloat16"),
-    "GT": ("sbuf", [128, 128], "bfloat16"), "LT": ("sbuf", [128, 128], "bfloat16"), "LB": ("sbuf", [128, 128], "bfloat16"),
+    "LB": ("sbuf", [128, 128], "bfloat16"), "CC": ("sbuf", [128, 16], "bfloat16"), "CF": ("sbuf", [128, 16], "bfloat16"),
     "CW": ("sbuf", [128, 144], "bfloat16"), "UW": ("sbuf", [128, 144], "bfloat16"), "RMK": ("sbuf", [128, 16], "float32"),
     "BR": ("sbuf", [128, 2048], "bfloat16"),
     "KC": ("sbuf", [128, 256], "float32"), "BS": ("sbuf", [128, 16], "float32"), "FC": ("sbuf", [128, 16], "float32"),
-    "DC": ("sbuf", [128, 128], "bfloat16"), "KD": ("sbuf", [128, 128], "float32"), "CL": ("sbuf", [128, 16], "uint16"),
+    "DC": ("sbuf", [128, 128], "bfloat16"), "KD": ("sbuf", [128, 256], "float32"), "CL": ("sbuf", [128, 16], "uint16"),
     "ZZ": ("sbuf", [128, 16], "bfloat16"),
     "XP": ("psum", [128, 2048], "float32"), "EP": ("psum", [128, 512], "float32"), "UP": ("psum", [128, 512], "float32"),
     "ZP": ("psum", [128, 512], "float32"), "SP": ("psum", [128, 512], "float32"),
@@ -53,7 +55,7 @@ for _t in range(ROUNDS):
     SCRATCH["SN%d" % _t] = ("sbuf", [128, SW], "bfloat16")
     SCRATCH["LD%d" % _t] = ("sbuf", [128, SW], "bfloat16")
 SEMAPHORES = (["qV", "qS", "qP", "qG", "loc"] + ["d%d" % i for i in range(6)]
-              + ["arr%d" % t for t in range(ROUNDS)] + ["hop%d" % t for t in range(ROUNDS)])
+              + ["%s%d" % (s, t) for s in ("arr", "hop") for t in range(ROUNDS)])
 
 
 def helpers(core, dst, topo):
@@ -90,10 +92,10 @@ def bridge(g, core, T, topo):
             if core not in hs:
                 continue
             lo, hi = parts_of(len(hs))[hs.index(core)]
-            k = len(topo.engines(src, core)) // len(hs)
-            g.wait_ge(T.sem["hop%d" % t], k)
+            g.wait_ge(T.sem["hop%d" % t], len(topo.engines(src, core)) // len(hs))
             rid, pid = topo.addr(dst, core)
-            g.remote_dma(T["LD%d" % t][:, lo:hi], T["LD%d" % t][:, lo:hi], T.sem["arr%d" % t], T.sem.loc, pid, rid, topo.mask(core, dst))
+            piece = T["LD%d" % t][:, lo:hi]
+            g.remote_dma(piece, piece, T.sem["arr%d" % t], T.sem.loc, pid, rid, topo.mask(core, dst))
             sent += len(topo.engines(core, dst))
     if sent:
         g.wait_ge(T.sem.loc, sent)
@@ -218,8 +220,8 @@ def rank_program(g, core, T, topo):
     def scatter(win, off, in_):
         run("V", lambda e: e.tensor_copy(win[1].indirect(off[1]), in_[1]), [win], [in_, off])
 
-    def scan(out, d0, d1, op0, op1):
-        run("V", lambda e: e.tensor_tensor_scan(out[1], d0[1], d1[1], 0.0, op0, op1), [out], [d0, d1])
+    def scan(out, d0, d1, op0, op1, initial=0.0):
+        run("V", lambda e: e.tensor_tensor_scan(out[1], d0[1], d1[1], initial, op0, op1), [out], [d0, d1])
 
     def fill(out, v):
         run("V", lambda e: e.memset(out[1], v), [out], [])
@@ -254,13 +256,12 @@ def rank_program(g, core, T, topo):
     iota(w("IG"), [[1, 8], [0, 16]], 0, 0)
     iota(w("IR"), [[1, 16]], 0, 0)
     iota(w("IM"), [[1, 128]], 0, 0)
+    iota(w("FC"), [[-16, 16]], 33024, 0)
     iota(w("DC"), [[0, 64], [-4096, 2]], 4096, 0)
-    iota(w("IK"), [[0, 8], [1, 16]], 0, 0)
-    iota(w("KC"), [[0, 16], [-256, 16]], 3840, 0)
+    iota(w("CC"), [[1, 16]], 0, 0)
+    iota(w("KC"), [[0, 16], [-2048, 16]], 30720, 0)
     iota(w("BS"), [[256, 16]], 240, 0)
-    iota(w("FC"), [[16, 16]], 4096, 0)
-    iota(w("IC"), [[1, 16]], 0, 0, False)
-    iota(c("TB", 2064, TW), [[0, TW - 2064]], 0, 0)
+    iota(w("IC"), [[16, 16]], 15, 0, False)
 
     ts(c("PC", 0, 1), c("PI", 0, 1), 4, A.arith_shift_right, 1, A.bitwise_and)
     ts(c("P4", 0, 1), c("PI", 0, 1), 4, A.arith_shift_right)
@@ -275,6 +276,9 @@ def rank_program(g, core, T, topo):
     podd, peven = c("PO", 0, 1), c("PE", 0, 1)
     ts(w("BD"), w("IG"), pg, A.is_equal)
     ts(w("RMK"), w("IR"), pr, A.is_equal)
+    ts(w("NBD"), w("BD"), -1.0, A.mult)
+    ts(c("PE", 1, 2), peven, 256.0, A.mult)
+    ts(c("PO", 1, 2), podd, 256.0, A.mult)
 
     def row_masks(lo, hi):
         for r in range(lo, hi):
@@ -292,18 +296,11 @@ def rank_program(g, core, T, topo):
     ts(w("I16"), w("IDN"), 16.0, A.mult)
     fill(w("ONE"), 1.0)
     fill(w("ZZ"), 0.0)
-    for k in range(2):
-        act(w("MS%d" % k), a("MKI", slice(None), slice(None), k), F.Copy, scale=4096.0)
-
-    def late_constants():
-        ts(w("N256"), w("IDN"), -256.0, A.mult)
-        ts(w("GT"), w("IM"), pp, A.is_gt)
-        ts(w("KD"), w("IK"), 0.5, A.is_gt)
-        tt(w("LT"), w("GT"), w("BD"), A.mult)
-        tt(w("LB"), w("LT"), w("BD"), A.subtract)
-        ts(w("BS"), w("BS"), pr, A.add)
-        ts(w("FC"), w("FC"), pr, A.add)
-        cp(w("CL"), w("IC"))
+    act(w("MS0"), a("MKI", slice(None), slice(None), 0), F.Copy, scale=4096.0)
+    fill(w("KD"), 1e9)
+    ts(c("KD", 0, 256, 16), w("FC"), pr, A.add)
+    run("G", lambda e: e.affine_select(w("LB")[1], w("NBD")[1], [[-1, 128]], A.is_ge, 0.0, 0, 1), [w("LB")], [w("NBD")])
+    iota(c("TB", 2064, TW), [[0, TW - 2064]], 0, 0)
 
     def expand(src3, second, first="V"):
         h0, h1 = slice(0, 16), slice(16, 32)
@@ -317,29 +314,38 @@ def rank_program(g, core, T, topo):
         turn(w("EY"), w("EX"))
         return a("EY", slice(None), slice(0, 16)), a("EY", slice(None), slice(16, 32))
 
-    def lines_of(cl):
-        every = slice(None)
-        tt(w("CB"), a("LEDI", every, every, cl), w("MS%d" % cl), A.add)
-        return w("CB")
-
-    def lists_turned(cl):
+    def class_0():
+        tt(w("CB"), a("LEDI", slice(None), slice(None), 0), w("MS0"), A.add)
+        expand(w("CB"), "S")
         h0, h1 = turned()
         tt(w("LL"), h0, h1, A.add)
-        if cl == 0:
-            ts(w("OFFM"), w("LL"), -4080.0, A.add)
-            fill(c("OFFM", 15, 256, 16), 8)
+        ts(w("OFFM"), w("LL"), -4080.0, A.add)
+        fill(c("OFFM", 15, 256, 16), 8)
         ts(w("M2"), w("LL"), 4095.5, A.is_ge, -4096.0, A.mult)
 
-    def take_lines(cl):
-        tt(w("E%d" % cl), w("LL"), w("M2"), A.add)
-        cp(w("OFF%d" % cl), w("E%d" % cl))
+    def class_0_lines():
+        tt(w("E0"), w("LL"), w("M2"), A.add)
+        cp(w("OFF0"), w("E0"))
 
-    def take_marks(cl):
-        ts(w("SG%d" % cl), w("M2"), 4.0, A.mult, 8192.0, A.add)
+    def marks_out(cl):
+        src = a("MKI", slice(None), slice(None), cl)
+        act(a("EXM", slice(None), slice(0, 16)), src, F.Copy, scale=c("PE", 1, 2))
+        act(a("EXM", slice(None), slice(16, 32)), src, F.Copy, scale=c("PO", 1, 2))
+
+    def marks_in(cl):
+        return [lambda: turn(w("EYM"), w("EXM")),
+                lambda: tt(w("MB%d" % cl), a("EYM", slice(None), slice(0, 16)), a("EYM", slice(None), slice(16, 32)), A.add),
+                lambda: act(w("SG%d" % cl), w("MB%d" % cl), F.Copy, scale=-512.0, bias=65536.0)]
+
+    def class_1_lines():
+        expand(a("LEDI", slice(None), slice(None), 1), "V")
+        h0, h1 = turned()
+        tt(w("E1"), h0, h1, A.add)
+        cp(w("OFF1"), w("E1"))
 
     def masks_of(cl, pairs):
         for i in pairs:
-            o = 512 * (i % 4)
+            o = 512 * ((i + 2) % 4)
             for k in (0, 1):
                 mm(c("XP", o + 256 * k, o + 256 * k + 256), c("BR", 128 * (2 * i + k), 128 * (2 * i + k) + 128), w("MB%d" % cl))
             for k in (0, 1):
@@ -381,15 +387,18 @@ def rank_program(g, core, T, topo):
             o = 512 * (b % 4)
             mm(c("XP", o, o + 512), w("IDN"), c("Q", 512 * b, 512 * b + 512))
 
-    def marked_gather(cl, q):
-        tt(quarter("MX", q), ind(items(), lists("OFF%d" % cl, q)), quarter("MM", q), A.min)
-        for k in range(4 * q, 4 * q + 4):
-            fill(c("MX", 256 * k + 240, 256 * k + 256), 4096.0)
+    def fused_list(cl):
+        ts(w("OFFX"), lists("E%d" % cl, 1), 16.0, A.add)
+        fill(c("OFFX", 15, 64, 16), 8)
+
+    def marked_gather(q):
+        tt(quarter("MX", q), ind(c("TB", 0, 2064), w("OFFX")), quarter("MM", q), A.min)
 
     def marked(q):
-        for k in range(4 * q, 4 * q + 4):
+        def one(k):
             o = 256 * (k % 8)
-            tt(c("MX", 256 * k, 256 * k + 240), c("XP", o, o + 240), c("MM", 256 * k, 256 * k + 240), A.min)
+            return lambda: tt(c("MX", 256 * k, 256 * k + 240), c("XP", o, o + 240), c("MM", 256 * k, 256 * k + 240), A.min)
+        return [one(k) for k in range(4 * q, 4 * q + 4)]
 
     def balances(h):
         for r in range(16):
@@ -410,24 +419,33 @@ def rank_program(g, core, T, topo):
         for r in range(16):
             mm(lists("ZP", q), c("CW", 15 - r, 143 - r), c("ZB", 1024 * q + r, 1024 * q + 1024, 16), r == 0, r == 15)
 
+    def scores(q):
+        return c("SP", 64 * q, 64 * q + 64) if q < 2 else c("XP", 512 * (q - 2), 512 * (q - 2) + 64)
+
     def score(q):
-        o = 64 * q if q < 2 else 320 + 64 * (q - 2)
         for r in range(16):
-            mm(c("SP" if q < 2 else "UP", o, o + 64), c("CW", 15 - r, 143 - r), c("DS", 1024 * q + r, 1024 * q + 1024, 16), r == 0, r == 15)
+            mm(scores(q), c("CW", 15 - r, 143 - r), c("DS", 1024 * q + r, 1024 * q + 1024, 16), r == 0, r == 15)
+
+    def weave(pattern, *steps):
+        its = [list(x) for x in steps]
+        for i in pattern:
+            its[i].pop(0)()
+        for x in its:
+            for f in x:
+                f()
 
     def hashes(h):
         s = (128 * h, 128 * h + 128)
-        cp(c("UI", *s), c("UP", *s))
-        ts(c("UM", *s), c("UI", *s), 2047, A.bitwise_and)
-        tt(c("PF", *s), c("UM", *s), c("EP", *s), A.mult)
-        tt(c("HI", *s), c("PF", *s), c("EP", 256 + s[0], 256 + s[1]), A.add)
-        ts(c("HH", *s), c("HI", *s), 5, A.arith_shift_right, 2047, A.bitwise_and)
-        cp(c("HO", *s), c("HH", *s))
+        return [lambda: cp(c("UI", *s), c("UP", *s)),
+                lambda: ts(c("UM", *s), c("UI", *s), 2047, A.bitwise_and),
+                lambda: tt(c("PF", *s), c("UM", *s), c("EP", *s), A.mult),
+                lambda: tt(c("HI", *s), c("PF", *s), c("EP", 256 + s[0], 256 + s[1]), A.add),
+                lambda: ts(c("HH", *s), c("HI", *s), 5, A.arith_shift_right, 2047, A.bitwise_and),
+                lambda: cp(c("HO", *s), c("HH", *s))]
 
     def low_keys(h):
         s = (128 * h, 128 * h + 128)
-        ts(c("UL", *s), c("UM", *s), 15, A.bitwise_and)
-        tt(c("KA", *s), c("UL", *s), c("KC", *s), A.add)
+        return [lambda: tt(c("KA", *s), c("UM", *s), c("SP", 256 + s[0], 256 + s[1]), A.add)]
 
     def over(q, eng):
         if eng == "S":
@@ -435,9 +453,9 @@ def rank_program(g, core, T, topo):
         else:
             ts(quarter("ZB", q), quarter("Q", q), 1.0, A.min)
 
-    def gate(cl, lo, hi):
-        ts(c("ZP", lo, hi), c("ZP", lo, hi), 8.5, A.is_ge)
-        tt(c("SGG", lo, hi), c("ZP", lo, hi), c("SG%d" % cl, lo, hi), A.mult)
+    def gate(lo, hi):
+        s = (lo, hi)
+        act(c("GG", *s), c("ZP", *s), F.Relu, scale=1048576.0, bias=-8388608.0)
 
     def far(q):
         act(quarter("D", q), ind(items(), lists("HO", q)), F.Copy)
@@ -458,21 +476,21 @@ def rank_program(g, core, T, topo):
         else:
             ts(quarter("DS", q), quarter("D", q), 1.0, A.min, -1.0, A.max)
 
-    def keys(h):
-        s = (128 * h, 128 * h + 128)
-        p = c("UP", 320, 448) if h else c("SP", 0, 128)
-        tt(p, p, c("SGG", *s), A.mult)
-        tt(c("KY", *s), p, c("KA", *s), A.add)
-        scan(c("RM", *s), w("KD"), c("KY", *s), A.mult, A.max)
+    def keys(cl, p, lo, hi):
+        s = (lo, hi)
+        return [lambda: tt(p, p, c("SG%d" % cl, *s), A.mult),
+                lambda: tt(p, p, c("GG", *s), A.min),
+                lambda: tt(c("KY", *s), p, c("KA", *s), A.add),
+                lambda: scan(c("RM", *s), c("KD", *s), c("KY", *s), A.min, A.max, 1e9)]
 
     def send(t):
         dst = T.cores[target(rank, t, n)]
         hs = helpers(core, dst, topo)
-        sn = w("SN%d" % t)
+        sn, ld = w("SN%d" % t), T["LD%d" % t]
         order("G", [sn], [])
         if not hs:
             rid, pid = topo.addr(dst, core)
-            g.remote_dma(T["LD%d" % t][:], sn[1], T.sem["arr%d" % t], T.sem.loc, pid, rid, topo.mask(core, dst))
+            g.remote_dma(ld[:], sn[1], T.sem["arr%d" % t], T.sem.loc, pid, rid, topo.mask(core, dst))
             return len(topo.engines(core, dst))
         tr, cnt = [], 0
         for i, (lo, hi) in enumerate(parts_of(len(hs))):
@@ -480,60 +498,60 @@ def rank_program(g, core, T, topo):
             k = len(es) // len(hs)
             rid, pid = topo.addr(hs[i], core)
             tr.append(RemoteDMATransfer(dst_ids=[DstId(rid=rid, pnc=pid)], dma_engine_mask=emask(es[i * k:(i + 1) * k]),
-                                        remote_sem=T.sem["hop%d" % t], srcs=[T["SN%d" % t][:, lo:hi]], dsts=[T["LD%d" % t][:, lo:hi]]))
+                                        remote_sem=T.sem["hop%d" % t], srcs=[T["SN%d" % t][:, lo:hi]], dsts=[ld[:, lo:hi]]))
             cnt += k
         g.remote_dma_fused(tr, local_sem=T.sem.loc)
         return cnt
 
-    def arrivals_of(t):
-        src = [r for r in range(n) if target(r, t, n) == rank][0]
-        hs = helpers(T.cores[src], core, topo)
-        cnt = sum(len(topo.engines(h, core)) for h in (hs or [T.cores[src]]))
-        note("R", "arr%d" % t, cnt, [], [w("LD%d" % t)], {})
-
     def winners(t):
-        tt(w("MP"), c("RM", 15, 256, 16), w("FC"), A.max)
-        cp(w("MI"), w("MP"))
-        ts(w("FL"), w("MP"), 8191.5, A.is_ge)
-        ts(w("EB"), w("MI"), 4, A.arith_shift_right, 240, A.bitwise_and)
+        best = c("RM", 15, 256, 16)
+        cp(w("MI"), best)
+        ts(w("FL"), best, 65535.5, A.is_ge)
+        ts(w("EB"), w("MI"), 7, A.arith_shift_right, 240, A.bitwise_and)
         scan(w("CU"), w("FL"), w("ZZ"), A.add, A.max)
         tt(w("IX"), w("BS"), w("EB"), A.subtract)
-        ts(w("S2"), w("MI"), 255, A.bitwise_and)
+        tt(w("CF"), w("FL"), w("CC"), A.mult)
         cp(w("IXU"), w("IX"))
-        pl = c("UP", 256, 272)
-        mm(pl, w("LB"), w("FL"), True, False)
+        ts(w("S2"), w("MI"), 15, A.bitwise_and)
+        pl = c("ZP", 256, 272)
+        mm(pl, w("IDN"), w("CC"), True, False)
+        mm(pl, w("LB"), w("FL"), False, False)
         mm(pl, w("N256"), w("FL"), False, False)
-        mm(pl, w("BD"), w("CU"), False, True)
+        mm(pl, w("BD"), w("CU"), False, False)
+        mm(pl, w("NID"), w("CF"), False, True)
         cp(c("SN%d" % t, 272, 288), w("S2"))
         cp(c("SN%d" % t, 0, 256), ind(w("Q"), w("IXU")))
-        act(c("SN%d" % t, 256, 272), pl, F.Copy)
+        cp(c("SN%d" % t, 256, 272), pl)
 
     def kappa():
         mm(c("UP", 288, 289), w("ONE"), c("CU", 15, 16))
-        ts(c("K1", 0, 1), c("UP", 288, 289), 32.0, A.mult)
-        ts(c("K2", 0, 1), c("K1", 0, 1), 1023, A.bitwise_and)
-        cp(c("K3", 0, 1), c("K2", 0, 1))
-
-    def flipped():
-        tt(w("WN"), ind(w("MP"), w("CL")), w("KY"), A.is_equal)
+        return [lambda: ts(c("K1", 0, 1), c("UP", 288, 289), 32.0, A.mult),
+                lambda: ts(c("K2", 0, 1), c("K1", 0, 1), 1023, A.bitwise_and),
+                lambda: cp(c("K3", 0, 1), c("K2", 0, 1))]
 
     def moves():
         tt(c("EP", 256, 512), w("HH"), c("EP", 0, 256), A.subtract)
 
-    def flips(cl):
-        e = w("E%d" % cl)
-        flipped()
-        act(c("ZP", 0, 256), w("WN"), F.Copy, scale=-2.0, bias=1.0)
-        tt(w("DW"), c("EP", 256, 512), w("WN"), A.mult)
-        tt(e, c("EP", 0, 256), w("DW"), A.add)
-        tt(w("SG%d" % cl), c("ZP", 0, 256), w("SG%d" % cl), A.mult)
+    def flips(cl, spread):
+        e, sg = w("E%d" % cl), w("SG%d" % cl)
+
+        def won():
+            tt(w("WN"), ind(w("RM"), w("CL")), w("KY"), A.is_equal)
+            if spread is not None:
+                masks_of(spread, range(PRE, 4))
+            act(c("ZP", 0, 256), w("WN"), F.Copy, scale=-2.0, bias=1.0)
+        return [won,
+                lambda: tt(w("DW"), c("EP", 256, 512), w("WN"), A.mult),
+                lambda: tt(e, c("EP", 0, 256), w("DW"), A.add),
+                lambda: tt(sg, c("ZP", 0, 256), sg, A.mult)]
 
     def renew(cl):
         cp(w("OFF%d" % cl), w("E%d" % cl))
-        act(w("MB%d" % cl), w("SG%d" % cl), F.Relu, scale=-255.0 / 8192.0)
+        act(w("MB%d" % cl), w("SG%d" % cl), F.Relu, scale=-1.0 / 256.0)
+        act(c("MB%d" % cl, 15, 256, 16), c("DC", 0, 32, 2), F.Copy)
 
     def last(cl):
-        ts(w("DW"), w("SG%d" % cl), -0.125, A.mult, 1024.0, A.add)
+        ts(w("DW"), w("SG%d" % cl), -1.0 / 64.0, A.mult, 1024.0, A.add)
         tt(w("LL"), w("DW"), w("E%d" % cl), A.add)
         expand(w("LL"), "V")
         h0, h1 = turned()
@@ -546,8 +564,10 @@ def rank_program(g, core, T, topo):
         tt(c("YLB", cl, 512, 2), w("OW"), m2, A.add)
 
     def apply(t):
-        arrivals_of(t)
+        src = T.cores[[r for r in range(n) if target(r, t, n) == rank][0]]
+        hs = helpers(src, core, topo)
         ld = "LD%d" % t
+        note("R", "arr%d" % t, sum(len(topo.engines(h, core)) for h in (hs or [src])), [], [w(ld)], {})
         of = c("UP", 272, 288)
         mm(of, w("I16"), c(ld, 256, 272), True, False)
         mm(of, w("IDN"), c(ld, 272, 288), False, True)
@@ -557,21 +577,22 @@ def rank_program(g, core, T, topo):
         scatter(c("TB", 16, TW), w("OU"), w("SH"))
 
     def first_half(cl):
-        gather_x(cl, 0, "S")
+        for i in (0, 1):
+            act(c("Q", 512 * i, 512 * i + 512), ind(items(), c("OFF%d" % cl, 32 * i, 32 * i + 32)), F.Copy)
         gather_x(cl, 1, "S")
-        marked_gather(cl, 1)
+        marked_gather(1)
         gather_x(cl, 2, "S")
         gather_x(cl, 3, "S")
         lift(0)
         lift(1)
-        marked(0)
+        weave((), marked(0))
         sum_u(0, 0)
         balances(0)
         odd_amounts(0)
 
     def first_half_0():
         gather_mx(0, "S")
-        take_lines(0)
+        class_0_lines()
         gather_mx(1, "V")
         gather_x(0, 0, "S")
         balances(0)
@@ -580,17 +601,18 @@ def rank_program(g, core, T, topo):
         gather_x(0, 2, "S")
         lift(0)
         lift(1)
-        take_marks(0)
-        lines_of(1)
-        late_constants()
+        ts(w("SG0"), w("M2"), 32.0, A.mult, 65536.0, A.add)
+        ts(w("N256"), w("IDN"), -256.0, A.mult)
+        ts(w("BS"), w("BS"), pr, A.add)
+        cp(w("CL"), w("IC"))
+        act(c("SP", 256, 512), w("KC"), F.Copy)
         sum_u(0, 0)
         gather_x(0, 3, "S")
         lines_to_psum(0, True)
         odd_amounts(0)
         gather_mx(3, "V")
 
-    expand(lines_of(0), "S")
-    lists_turned(0)
+    class_0()
     total = 0
     for t in range(ROUNDS):
         cl, nx = t % 2, 1 - t % 2
@@ -599,75 +621,69 @@ def rank_program(g, core, T, topo):
             first_half(cl)
         else:
             first_half_0()
-        lift(2)
         sum_u(0, 1)
+        lift(2)
         over(0, "V")
         over(1, "S")
         if t:
-            marked(2)
+            weave((1, 1, 1, 0, 1), hashes(0), marked(2))
+            lift(3)
+            weave((), marked(3))
         else:
-            expand(w("CB"), "S", "S")
+            marks_out(1)
             row_masks(8, 16)
-        lift(3)
-        hashes(0)
-        if t:
-            marked(3)
+            lift(3)
+            weave((), hashes(0))
         count_over(0)
         count_over(1)
         sum_u(1, 0)
         far(0)
+        gate(0, 128)
         far(1)
         balances(1)
         odd_amounts(1)
         sum_u(1, 1)
-        low_keys(0)
         for b in range(4):
             minus(b, bank[b])
         over(2, "S")
-        hashes(1)
-        for b in range(2):
+        weave((1, 0, 0, 2, 0, 2, 0), hashes(1), low_keys(0), marks_in(1) if t == 0 else [lambda: None] * 2)
+        for b in range(4):
             sign_psum(b, bank[b])
-        over(3, "S")
-        for b in range(2, 4):
-            sign_psum(b, bank[b])
-        if t == 0:
-            lists_turned(1)
-            ts(w("MB1"), w("M2"), -255.0 / 4096.0, A.mult)
         diff(2)
         count_over(2)
         score(0)
-        count_over(3)
         score(1)
+        gate(128, 192)
         sign(2, "S")
+        over(3, "S")
         diff(3)
         sign(3, "V")
-        low_keys(1)
-        gate(cl, 0, 256)
+        if t == 0:
+            fill(c("MB1", 15, 256, 16), 4096.0)
         score(2)
-        keys(0)
+        weave((0, 1, 0), keys(cl, c("SP", 0, 128), 0, 128), low_keys(1))
         score(3)
+        count_over(3)
+        gate(192, 256)
         if t + 1 < ROUNDS:
             masks_of(nx, range(PRE))
-        moves()
-        if t + 1 == ROUNDS:
-            out_columns(nx)
-        keys(1)
+        weave((0, 0, 1, 0, 1, 0, 1, 1), keys(cl, scores(2), 128, 192), keys(cl, scores(3), 192, 256))
         winners(t)
         total += send(t)
-        if t + 1 < ROUNDS:
-            kappa()
+        moves()
         if t == 0:
-            take_lines(1)
-            take_marks(1)
-        flips(cl)
+            class_1_lines()
+        weave((1, 0, 1, 0, 1, 0, 1), *((kappa(), flips(cl, nx)) if t + 1 < ROUNDS else ([lambda: None] * 3, flips(cl, None))))
         if t + 1 < ROUNDS:
-            masks_of(nx, range(PRE, 8))
+            masks_of(nx, range(4, 8))
+            lines_to_psum(nx, False)
+            fused_list(nx)
         if t + 2 < ROUNDS:
             renew(cl)
         else:
             last(cl)
-        if t + 1 < ROUNDS:
-            lines_to_psum(nx, False)
+        if t + 2 == ROUNDS:
+            out_columns(cl)
         apply(t)
     dma("Y", "d5", T.yx[:], items())
     out_columns(cl)

import numpy as np
from concourse.bass import DstId, RemoteDMATransfer
from concourse.mybir import dt, AluOpType, AxisListType, ActivationFunctionType

ROUNDS = 4
PRE = 2
SW = 288
TW = 8448
SCRATCH = {
    "TB": ("sbuf", [128, TW], "bfloat16"),
    "LEDI": ("sbuf", [128, 16, 16, 2], "int32"), "MKI": ("sbuf", [128, 16, 16, 2], "bfloat16"),
    "MS0": ("sbuf", [128, 16, 16], "float32"), "CB": ("sbuf", [128, 16, 16], "float32"), "OFFM": ("sbuf", [128, 256], "uint16"),
    "OFFX": ("sbuf", [128, 64], "uint16"),
    "EX": ("sbuf", [128, 16, 32], "float32"), "EY": ("sbuf", [128, 16, 32], "float32"),
    "LL": ("sbuf", [128, 16, 16], "float32"), "M2": ("sbuf", [128, 256], "float32"),
    "YLB": ("sbuf", [128, 512], "float32"), "YMB": ("sbuf", [128, 512], "bfloat16"),
    "Q": ("sbuf", [128, 4096], "bfloat16"), "MX": ("sbuf", [128, 4096], "bfloat16"), "SB": ("sbuf", [128, 4096], "bfloat16"),
    "D": ("sbuf", [128, 4096], "bfloat16"), "ZB": ("sbuf", [128, 4096], "bfloat16"), "DS": ("sbuf", [128, 4096], "bfloat16"),
    "MM": ("sbuf", [128, 4096], "bfloat16"),
    "UI": ("sbuf", [128, 256], "int32"), "UM": ("sbuf", [128, 256], "int32"), "PF": ("sbuf", [128, 256], "float32"),
    "HI": ("sbuf", [128, 256], "int32"), "HH": ("sbuf", [128, 256], "int32"), "HO": ("sbuf", [128, 256], "uint16"),
    "UL": ("sbuf", [128, 256], "int32"), "KA": ("sbuf", [128, 256], "float32"), "GG": ("sbuf", [128, 256], "float32"),
    "KY": ("sbuf", [128, 256], "float32"), "RM": ("sbuf", [128, 256], "float32"),
    "MI": ("sbuf", [128, 16], "int32"), "EB": ("sbuf", [128, 16], "int32"), "FL": ("sbuf", [128, 16], "bfloat16"),
    "CU": ("sbuf", [128, 16], "bfloat16"), "IX": ("sbuf", [128, 16], "int32"), "IXU": ("sbuf", [128, 16], "uint16"),
    "S2": ("sbuf", [128, 16], "int32"), "OU": ("sbuf", [128, 16], "uint16"),
    "SM": ("sbuf", [128, 256], "int32"), "SH": ("sbuf", [128, 256], "int32"),
    "WN": ("sbuf", [128, 256], "float32"), "W2": ("sbuf", [128, 256], "float32"), "DE": ("sbuf", [128, 256], "float32"),
    "DW": ("sbuf", [128, 256], "float32"), "OW": ("sbuf", [128, 256], "float32"),
    "K1": ("sbuf", [128, 8], "int32"), "K2": ("sbuf", [128, 8], "int32"), "K3": ("sbuf", [128, 8], "float32"),
    "PI": ("sbuf", [128, 8], "int32"), "P4": ("sbuf", [128, 8], "int32"), "P15": ("sbuf", [128, 8], "int32"),
    "PC": ("sbuf", [128, 8], "int32"), "PF1": ("sbuf", [128, 8], "float32"), "PG": ("sbuf", [128, 8], "float32"),
    "PR": ("sbuf", [128, 8], "float32"), "PW": ("sbuf", [128, 8], "float32"), "PO": ("sbuf", [128, 8], "float32"),
    "PE": ("sbuf", [128, 8], "float32"),
    "IM": ("sbuf", [128, 128], "float32"), "IG": ("sbuf", [128, 128], "float32"), "IR": ("sbuf", [128, 16], "float32"),
    "IC": ("sbuf", [128, 16], "int32"), "NBD": ("sbuf", [128, 128], "bfloat16"),
    "EXM": ("sbuf", [128, 16, 32], "bfloat16"), "EYM": ("sbuf", [128, 16, 32], "bfloat16"),
    "BD": ("sbuf", [128, 128], "bfloat16"), "IDN": ("sbuf", [128, 128], "bfloat16"), "NID": ("sbuf", [128, 128], "bfloat16"),
    "I16": ("sbuf", [128, 128], "bfloat16"), "N256": ("sbuf", [128, 128], "bfloat16"), "ONE": ("sbuf", [128, 128], "bfloat16"),
    "LB": ("sbuf", [128, 128], "bfloat16"), "CC": ("sbuf", [128, 16], "bfloat16"), "CF": ("sbuf", [128, 16], "bfloat16"),
    "CW": ("sbuf", [128, 144], "bfloat16"), "UW": ("sbuf", [128, 144], "bfloat16"), "RMK": ("sbuf", [128, 16], "float32"),
    "BR": ("sbuf", [128, 2048], "bfloat16"),
    "KC": ("sbuf", [128, 256], "float32"), "BS": ("sbuf", [128, 16], "float32"), "FC": ("sbuf", [128, 16], "float32"),
    "DC": ("sbuf", [128, 128], "bfloat16"), "KD": ("sbuf", [128, 256], "float32"), "CL": ("sbuf", [128, 16], "uint16"),
    "ZZ": ("sbuf", [128, 16], "bfloat16"),
    "XP": ("psum", [128, 2048], "float32"), "EP": ("psum", [128, 512], "float32"), "UP": ("psum", [128, 512], "float32"),
    "ZP": ("psum", [128, 512], "float32"), "SP": ("psum", [128, 512], "float32"),
}
for _c in range(2):
    SCRATCH["OFF%d" % _c] = ("sbuf", [128, 256], "uint16")
    SCRATCH["E%d" % _c] = ("sbuf", [128, 256], "float32")
    SCRATCH["SG%d" % _c] = ("sbuf", [128, 256], "float32")
    SCRATCH["MB%d" % _c] = ("sbuf", [128, 256], "bfloat16")
for _t in range(ROUNDS):
    SCRATCH["SN%d" % _t] = ("sbuf", [128, SW], "bfloat16")
    SCRATCH["LD%d" % _t] = ("sbuf", [128, SW], "bfloat16")
SEMAPHORES = (["qV", "qS", "qP", "qG", "loc"] + ["d%d" % i for i in range(6)]
              + ["%s%d" % (s, t) for s in ("arr", "hop") for t in range(ROUNDS)])


def helpers(core, dst, topo):
    if topo.may_write(core, dst):
        return []
    own = [c for c in topo.cores_of(core) if c != core and topo.may_write(c, dst)]
    near = [c for c in own if topo.die(c) == topo.die(core)]
    return (near or own)[:2]


def target(rank, t, n):
    return (rank + 1 + t % (n - 1)) % n


def emask(engines):
    m = 0
    for e in engines:
        m |= 1 << e
    return m


def parts_of(n):
    w = SW // n
    return [(i * w, (i + 1) * w) for i in range(n)]


def bridge(g, core, T, topo):
    n = len(T.cores)
    sent = 0
    for t in range(ROUNDS):
        for r in range(n):
            src, dst = T.cores[r], T.cores[target(r, t, n)]
            hs = helpers(src, dst, topo)
            if core not in hs:
                continue
            lo, hi = parts_of(len(hs))[hs.index(core)]
            g.wait_ge(T.sem["hop%d" % t], len(topo.engines(src, core)) // len(hs))
            rid, pid = topo.addr(dst, core)
            piece = T["LD%d" % t][:, lo:hi]
            g.remote_dma(piece, piece, T.sem["arr%d" % t], T.sem.loc, pid, rid, topo.mask(core, dst))
            sent += len(topo.engines(core, dst))
    if sent:
        g.wait_ge(T.sem.loc, sent)


def rank_program(g, core, T, topo):
    rank = T.rank_of(core)
    if rank is None:
        bridge(g, core, T, topo)
        return
    A, F = AluOpType, ActivationFunctionType
    n = len(T.cores)
    Qs = {"V": g.vector, "S": g.scalar, "P": g.tensor, "G": g, "Y": g.sync}
    seq = {"V": 0, "S": 0, "P": 0, "G": 0}
    known = {q: {} for q in Qs}
    log = {}
    masks = {}

    def a(name, *idx):
        key = (name, str(idx))
        if key not in masks:
            shape = SCRATCH[name][1][1:]
            bits = np.zeros(int(np.prod(shape)), np.uint8)
            ids = np.arange(bits.size).reshape(shape)
            bits[(ids[idx] if idx else ids).ravel()] = 1
            exact = int.from_bytes(np.packbits(bits).tobytes(), "big")
            bank = exact
            if SCRATCH[name][0] == "psum":
                wide = bits.copy()
                for b in range(0, bits.size, 512):
                    if bits[b:b + 512].any():
                        wide[b:b + 512] = 1
                bank = int.from_bytes(np.packbits(wide).tobytes(), "big")
            masks[key] = (exact, bank)
        return (name, T[name][(slice(None),) + tuple(idx)], masks[key][0], masks[key][1])

    def c(name, lo, hi, step=1):
        return a(name, slice(lo, hi, step) if step != 1 else slice(lo, hi))

    def w(name):
        return a(name)

    def order(q, reads, writes):
        need = {}
        for isw, lst in ((False, reads), (True, writes)):
            for name, _, ex, bk in lst:
                psum = SCRATCH[name][0] == "psum"
                for rq, src, cnt, rw, rex, rbk, clk in log.get(name, []):
                    if psum and rq != q:
                        hit = bk & rbk
                    elif psum and q == "P":
                        hit = 0
                    else:
                        hit = (isw or rw) and (ex & rex)
                    if hit and need.get(src, (0, None))[0] < cnt:
                        need[src] = (cnt, clk)
        for src in sorted(need, key=lambda s: -len(need[s][1])):
            cnt, clk = need[src]
            if known[q].get(src, 0) < cnt:
                Qs[q].wait_ge(T.sem[src], cnt)
                for s, v in clk.items():
                    known[q][s] = max(known[q].get(s, 0), v)
                known[q][src] = max(known[q].get(src, 0), cnt)

    def note(q, src, cnt, reads, writes, clk):
        for isw, lst in ((False, reads), (True, writes)):
            for name, _, ex, bk in lst:
                old = log.get(name, [])
                if isw:
                    old = [x for x in old if x[4] & ~ex]
                old.append((q, src, cnt, isw, ex, bk, clk))
                log[name] = old

    def run(q, fn, writes, reads):
        order(q, reads, writes)
        src = "q" + q
        fn(Qs[q]).then_inc(T.sem[src], 1)
        seq[q] += 1
        clk = dict(known[q])
        clk[src] = seq[q]
        note(q, src, seq[q], reads, writes, clk)

    def dma(q, sem, out, in_):
        reads = [in_] if isinstance(in_, tuple) else []
        writes = [out] if isinstance(out, tuple) else []
        order(q, reads, writes)
        Qs[q].dma_start(out[1] if writes else out, in_[1] if reads else in_).then_inc(T.sem[sem], 16)
        note(q, sem, 16, reads, writes, dict(known[q]))

    def ind(win, off):
        return ("ind", win, off)

    def opnd(x, reads):
        if x[0] == "ind":
            reads += [x[1], x[2]]
            return x[1][1].indirect(x[2][1])
        reads.append(x)
        return x[1]

    def sc(x, reads):
        return opnd(x, reads) if isinstance(x, tuple) else x

    def tt(out, in0, in1, op):
        r = []
        i0, i1 = opnd(in0, r), opnd(in1, r)
        run("V", lambda e: e.tensor_tensor(out[1], i0, i1, op), [out], r)

    def ts(out, in0, s1, op0, s2=None, op1=None):
        r = []
        i0, x1 = opnd(in0, r), sc(s1, r)
        if op1 is None:
            run("V", lambda e: e.tensor_scalar(out[1], i0, x1, None, op0), [out], r)
        else:
            x2 = sc(s2, r)
            run("V", lambda e: e.tensor_scalar(out[1], i0, x1, x2, op0, op1), [out], r)

    def cp(out, in_):
        r = []
        i0 = opnd(in_, r)
        run("V", lambda e: e.tensor_copy(out[1], i0), [out], r)

    def scatter(win, off, in_):
        run("V", lambda e: e.tensor_copy(win[1].indirect(off[1]), in_[1]), [win], [in_, off])

    def scan(out, d0, d1, op0, op1, initial=0.0):
        run("V", lambda e: e.tensor_tensor_scan(out[1], d0[1], d1[1], initial, op0, op1), [out], [d0, d1])

    def fill(out, v):
        run("V", lambda e: e.memset(out[1], v), [out], [])

    def turn(out, in_):
        run("V", lambda e: e.transpose(out[1], in_[1]), [out], [in_])

    def act(out, in_, func, scale=None, bias=None):
        r = []
        i0 = opnd(in_, r)
        kw = {}
        if scale is not None:
            kw["scale"] = sc(scale, r)
        if bias is not None:
            kw["bias"] = sc(bias, r)
        run("S", lambda e: e.activation(out[1], i0, func, **kw), [out], r)

    def mm(out, lhsT, rhs, start=True, stop=True):
        run("P", lambda e: e.matmul(out[1], lhsT[1], rhs[1], start, stop), [out], [lhsT, rhs])

    def iota(out, pattern, base, cm, flag=True):
        if flag:
            run("G", lambda e: e.iota(out[1], pattern, base, cm, allow_small_or_imprecise_dtypes=True), [out], [])
        else:
            run("G", lambda e: e.iota(out[1], pattern, base, cm), [out], [])

    dma("Y", "d0", w("LEDI"), T.led[:])
    dma("S", "d1", w("MKI"), T.mk[:])
    dma("Y", "d2", c("TB", 16, 2064), T.xt[:])

    iota(c("PI", 0, 1), [[0, 1]], 0, 1, False)
    iota(w("IG"), [[1, 8], [0, 16]], 0, 0)
    iota(w("IR"), [[1, 16]], 0, 0)
    iota(w("IM"), [[1, 128]], 0, 0)
    iota(w("FC"), [[-16, 16]], 33024, 0)
    iota(w("DC"), [[0, 64], [-4096, 2]], 4096, 0)
    iota(w("CC"), [[1, 16]], 0, 0)
    iota(w("KC"), [[0, 16], [-2048, 16]], 30720, 0)
    iota(w("BS"), [[256, 16]], 240, 0)
    iota(w("IC"), [[16, 16]], 15, 0, False)

    ts(c("PC", 0, 1), c("PI", 0, 1), 4, A.arith_shift_right, 1, A.bitwise_and)
    ts(c("P4", 0, 1), c("PI", 0, 1), 4, A.arith_shift_right)
    ts(c("P15", 0, 1), c("PI", 0, 1), 15, A.bitwise_and)
    cp(c("PO", 0, 1), c("PC", 0, 1))
    ts(c("PE", 0, 1), c("PC", 0, 1), -1.0, A.mult, 1.0, A.add)
    cp(c("PG", 0, 1), c("P4", 0, 1))
    cp(c("PR", 0, 1), c("P15", 0, 1))
    cp(c("PF1", 0, 1), c("PI", 0, 1))
    ts(c("PW", 0, 1), c("P15", 0, 1), 2.0, A.mult, 1.0, A.add)
    pg, pr, pp, pw = c("PG", 0, 1), c("PR", 0, 1), c("PF1", 0, 1), c("PW", 0, 1)
    podd, peven = c("PO", 0, 1), c("PE", 0, 1)
    ts(w("BD"), w("IG"), pg, A.is_equal)
    ts(w("RMK"), w("IR"), pr, A.is_equal)
    ts(w("NBD"), w("BD"), -1.0, A.mult)
    ts(c("PE", 1, 2), peven, 256.0, A.mult)
    ts(c("PO", 1, 2), podd, 256.0, A.mult)

    def row_masks(lo, hi):
        for r in range(lo, hi):
            act(c("BR", 128 * r, 128 * r + 128), w("BD"), F.Copy, scale=c("RMK", r, r + 1))

    row_masks(0, 8)
    fill(c("TB", 0, 8), 0.0)
    fill(c("TB", 8, 16), 4096.0)
    ts(w("IDN"), w("IM"), pp, A.is_equal)
    fill(w("CW"), 0.0)
    ts(c("CW", 15, 143, 16), c("IG", 0, 128, 16), pg, A.is_equal)
    ts(w("UW"), w("CW"), pw, A.mult)

    ts(w("NID"), w("IDN"), -1.0, A.mult)
    ts(w("I16"), w("IDN"), 16.0, A.mult)
    fill(w("ONE"), 1.0)
    fill(w("ZZ"), 0.0)
    act(w("MS0"), a("MKI", slice(None), slice(None), 0), F.Copy, scale=4096.0)
    fill(w("KD"), 1e9)
    ts(c("KD", 0, 256, 16), w("FC"), pr, A.add)
    run("G", lambda e: e.affine_select(w("LB")[1], w("NBD")[1], [[-1, 128]], A.is_ge, 0.0, 0, 1), [w("LB")], [w("NBD")])
    iota(c("TB", 2064, TW), [[0, TW - 2064]], 0, 0)

    def expand(src3, second, first="V"):
        h0, h1 = slice(0, 16), slice(16, 32)
        for h, eng, col in ((h0, first, peven), (h1, second, podd)):
            if eng == "S":
                act(a("EX", slice(None), h), src3, F.Copy, scale=col)
            else:
                ts(a("EX", slice(None), h), src3, col, A.mult)

    def turned():
        turn(w("EY"), w("EX"))
        return a("EY", slice(None), slice(0, 16)), a("EY", slice(None), slice(16, 32))

    def class_0():
        tt(w("CB"), a("LEDI", slice(None), slice(None), 0), w("MS0"), A.add)
        expand(w("CB"), "S")
        h0, h1 = turned()
        tt(w("LL"), h0, h1, A.add)
        ts(w("OFFM"), w("LL"), -4080.0, A.add)
        fill(c("OFFM", 15, 256, 16), 8)
        ts(w("M2"), w("LL"), 4095.5, A.is_ge, -4096.0, A.mult)

    def class_0_lines():
        tt(w("E0"), w("LL"), w("M2"), A.add)
        cp(w("OFF0"), w("E0"))

    def marks_out(cl):
        src = a("MKI", slice(None), slice(None), cl)
        act(a("EXM", slice(None), slice(0, 16)), src, F.Copy, scale=c("PE", 1, 2))
        act(a("EXM", slice(None), slice(16, 32)), src, F.Copy, scale=c("PO", 1, 2))

    def marks_in(cl):
        return [lambda: turn(w("EYM"), w("EXM")),
                lambda: tt(w("MB%d" % cl), a("EYM", slice(None), slice(0, 16)), a("EYM", slice(None), slice(16, 32)), A.add),
                lambda: act(w("SG%d" % cl), w("MB%d" % cl), F.Copy, scale=-512.0, bias=65536.0)]

    def class_1_lines():
        expand(a("LEDI", slice(None), slice(None), 1), "V")
        h0, h1 = turned()
        tt(w("E1"), h0, h1, A.add)
        cp(w("OFF1"), w("E1"))

    def masks_of(cl, pairs):
        for i in pairs:
            o = 512 * ((i + 2) % 4)
            for k in (0, 1):
                mm(c("XP", o + 256 * k, o + 256 * k + 256), c("BR", 128 * (2 * i + k), 128 * (2 * i + k) + 128), w("MB%d" % cl))
            for k in (0, 1):
                act(c("MM", 2 * i + k, 4096, 16), c("XP", o + 256 * k, o + 256 * k + 256), F.Copy)

    def lines_to_psum(cl, first):
        e = w("E%d" % cl)
        act(c("EP", 0, 256), e, F.Copy)
        if first:
            act(c("EP", 256, 512), e, F.Copy, scale=32.0)
        else:
            act(c("EP", 256, 512), e, F.Identity, scale=32.0, bias=c("K3", 0, 1))

    def items():
        return c("TB", 16, 2064)

    def quarter(name, q):
        return c(name, 1024 * q, 1024 * q + 1024)

    def lists(name, q):
        return c(name, 64 * q, 64 * q + 64)

    def gather_x(cl, q, eng):
        src = ind(items(), lists("OFF%d" % cl, q))
        if eng == "S":
            act(quarter("Q", q), src, F.Copy)
        else:
            cp(quarter("Q", q), src)

    def gather_mx(q, eng):
        src = ind(c("TB", 0, 2064), lists("OFFM", q))
        if eng == "S":
            act(quarter("MX", q), src, F.Copy)
        else:
            cp(quarter("MX", q), src)

    def lift(q):
        for b in (2 * q, 2 * q + 1):
            o = 512 * (b % 4)
            mm(c("XP", o, o + 512), w("IDN"), c("Q", 512 * b, 512 * b + 512))

    def fused_list(cl):
        ts(w("OFFX"), lists("E%d" % cl, 1), 16.0, A.add)
        fill(c("OFFX", 15, 64, 16), 8)

    def marked_gather(q):
        tt(quarter("MX", q), ind(c("TB", 0, 2064), w("OFFX")), quarter("MM", q), A.min)

    def marked(q):
        def one(k):
            o = 256 * (k % 8)
            return lambda: tt(c("MX", 256 * k, 256 * k + 240), c("XP", o, o + 240), c("MM", 256 * k, 256 * k + 240), A.min)
        return [one(k) for k in range(4 * q, 4 * q + 4)]

    def balances(h):
        for r in range(16):
            lo, hi = 2048 * h + r, 2048 * h + 2048
            scan(c("SB", lo, hi, 16), c("MX", lo, hi, 16), w("DC"), A.subtract, A.min)

    def odd_amounts(h):
        for r in range(16):
            lo, hi = 2048 * h + r, 2048 * h + 2048
            tt(c("Q", lo + 16, hi, 32), c("XP", 16 + r, 2048, 32), c("SB", lo, hi, 32), A.min)

    def sum_u(h, odd):
        for r in range(16):
            lo, hi = 2048 * h + r + 16 * odd, 2048 * h + 2048
            mm(c("UP", 128 * h + odd, 128 * h + 128, 2), c("UW", 15 - r, 143 - r), c("Q", lo, hi, 32), r == 0, r == 15)

    def count_over(q):
        for r in range(16):
            mm(lists("ZP", q), c("CW", 15 - r, 143 - r), c("ZB", 1024 * q + r, 1024 * q + 1024, 16), r == 0, r == 15)

    def scores(q):
        return c("SP", 64 * q, 64 * q + 64) if q < 2 else c("XP", 512 * (q - 2), 512 * (q - 2) + 64)

    def score(q):
        for r in range(16):
            mm(scores(q), c("CW", 15 - r, 143 - r), c("DS", 1024 * q + r, 1024 * q + 1024, 16), r == 0, r == 15)

    def weave(pattern, *steps):
        its = [list(x) for x in steps]
        for i in pattern:
            its[i].pop(0)()
        for x in its:
            for f in x:
                f()

    def hashes(h):
        s = (128 * h, 128 * h + 128)
        return [lambda: cp(c("UI", *s), c("UP", *s)),
                lambda: ts(c("UM", *s), c("UI", *s), 2047, A.bitwise_and),
                lambda: tt(c("PF", *s), c("UM", *s), c("EP", *s), A.mult),
                lambda: tt(c("HI", *s), c("PF", *s), c("EP", 256 + s[0], 256 + s[1]), A.add),
                lambda: ts(c("HH", *s), c("HI", *s), 5, A.arith_shift_right, 2047, A.bitwise_and),
                lambda: cp(c("HO", *s), c("HH", *s))]

    def low_keys(h):
        s = (128 * h, 128 * h + 128)
        return [lambda: tt(c("KA", *s), c("UM", *s), c("SP", 256 + s[0], 256 + s[1]), A.add)]

    def over(q, eng):
        if eng == "S":
            act(quarter("ZB", q), quarter("Q", q), F.Sign)
        else:
            ts(quarter("ZB", q), quarter("Q", q), 1.0, A.min)

    def gate(lo, hi):
        s = (lo, hi)
        act(c("GG", *s), c("ZP", *s), F.Relu, scale=1048576.0, bias=-8388608.0)

    def far(q):
        act(quarter("D", q), ind(items(), lists("HO", q)), F.Copy)

    def minus(b, out):
        mm(out, w("IDN"), c("D", 512 * b, 512 * b + 512), True, False)
        mm(out, w("NID"), c("Q", 512 * b, 512 * b + 512), False, True)

    def sign_psum(b, src):
        act(c("DS", 512 * b, 512 * b + 512), src, F.Sign)

    def diff(q):
        tt(quarter("D", q), ind(items(), lists("HO", q)), quarter("Q", q), A.subtract)

    def sign(q, eng):
        if eng == "S":
            act(quarter("DS", q), quarter("D", q), F.Sign)
        else:
            ts(quarter("DS", q), quarter("D", q), 1.0, A.min, -1.0, A.max)

    def keys(cl, p, lo, hi):
        s = (lo, hi)
        return [lambda: tt(p, p, c("SG%d" % cl, *s), A.mult),
                lambda: tt(p, p, c("GG", *s), A.min),
                lambda: tt(c("KY", *s), p, c("KA", *s), A.add),
                lambda: scan(c("RM", *s), c("KD", *s), c("KY", *s), A.min, A.max, 1e9)]

    def send(t):
        dst = T.cores[target(rank, t, n)]
        hs = helpers(core, dst, topo)
        sn, ld = w("SN%d" % t), T["LD%d" % t]
        order("G", [sn], [])
        if not hs:
            rid, pid = topo.addr(dst, core)
            g.remote_dma(ld[:], sn[1], T.sem["arr%d" % t], T.sem.loc, pid, rid, topo.mask(core, dst))
            return len(topo.engines(core, dst))
        tr, cnt = [], 0
        for i, (lo, hi) in enumerate(parts_of(len(hs))):
            es = topo.engines(core, hs[i])
            k = len(es) // len(hs)
            rid, pid = topo.addr(hs[i], core)
            tr.append(RemoteDMATransfer(dst_ids=[DstId(rid=rid, pnc=pid)], dma_engine_mask=emask(es[i * k:(i + 1) * k]),
                                        remote_sem=T.sem["hop%d" % t], srcs=[T["SN%d" % t][:, lo:hi]], dsts=[ld[:, lo:hi]]))
            cnt += k
        g.remote_dma_fused(tr, local_sem=T.sem.loc)
        return cnt

    def winners(t):
        best = c("RM", 15, 256, 16)
        cp(w("MI"), best)
        ts(w("FL"), best, 65535.5, A.is_ge)
        ts(w("EB"), w("MI"), 7, A.arith_shift_right, 240, A.bitwise_and)
        scan(w("CU"), w("FL"), w("ZZ"), A.add, A.max)
        tt(w("IX"), w("BS"), w("EB"), A.subtract)
        tt(w("CF"), w("FL"), w("CC"), A.mult)
        cp(w("IXU"), w("IX"))
        ts(w("S2"), w("MI"), 15, A.bitwise_and)
        pl = c("ZP", 256, 272)
        mm(pl, w("IDN"), w("CC"), True, False)
        mm(pl, w("LB"), w("FL"), False, False)
        mm(pl, w("N256"), w("FL"), False, False)
        mm(pl, w("BD"), w("CU"), False, False)
        mm(pl, w("NID"), w("CF"), False, True)
        cp(c("SN%d" % t, 272, 288), w("S2"))
        cp(c("SN%d" % t, 0, 256), ind(w("Q"), w("IXU")))
        cp(c("SN%d" % t, 256, 272), pl)

    def kappa():
        mm(c("UP", 288, 289), w("ONE"), c("CU", 15, 16))
        return [lambda: ts(c("K1", 0, 1), c("UP", 288, 289), 32.0, A.mult),
                lambda: ts(c("K2", 0, 1), c("K1", 0, 1), 1023, A.bitwise_and),
                lambda: cp(c("K3", 0, 1), c("K2", 0, 1))]

    def moves():
        tt(c("EP", 256, 512), w("HH"), c("EP", 0, 256), A.subtract)

    def flips(cl, spread):
        e, sg = w("E%d" % cl), w("SG%d" % cl)

        def won():
            tt(w("WN"), ind(w("RM"), w("CL")), w("KY"), A.is_equal)
            if spread is not None:
                masks_of(spread, range(PRE, 4))
            act(c("ZP", 0, 256), w("WN"), F.Copy, scale=-2.0, bias=1.0)
        return [won,
                lambda: tt(w("DW"), c("EP", 256, 512), w("WN"), A.mult),
                lambda: tt(e, c("EP", 0, 256), w("DW"), A.add),
                lambda: tt(sg, c("ZP", 0, 256), sg, A.mult)]

    def renew(cl):
        cp(w("OFF%d" % cl), w("E%d" % cl))
        act(w("MB%d" % cl), w("SG%d" % cl), F.Relu, scale=-1.0 / 256.0)
        act(c("MB%d" % cl, 15, 256, 16), c("DC", 0, 32, 2), F.Copy)

    def last(cl):
        ts(w("DW"), w("SG%d" % cl), -1.0 / 64.0, A.mult, 1024.0, A.add)
        tt(w("LL"), w("DW"), w("E%d" % cl), A.add)
        expand(w("LL"), "V")
        h0, h1 = turned()
        tt(w("OW"), h0, h1, A.add)

    def out_columns(cl):
        m2 = w("M2")
        ts(m2, w("OW"), 2047.5, A.is_ge, -2048.0, A.mult)
        act(c("YMB", cl, 512, 2), m2, F.Copy, scale=-1.0 / 2048.0)
        tt(c("YLB", cl, 512, 2), w("OW"), m2, A.add)

    def apply(t):
        src = T.cores[[r for r in range(n) if target(r, t, n) == rank][0]]
        hs = helpers(src, core, topo)
        ld = "LD%d" % t
        note("R", "arr%d" % t, sum(len(topo.engines(h, core)) for h in (hs or [src])), [], [w(ld)], {})
        of = c("UP", 272, 288)
        mm(of, w("I16"), c(ld, 256, 272), True, False)
        mm(of, w("IDN"), c(ld, 272, 288), False, True)
        ts(w("OU"), of, 4096.0, A.add)
        tt(w("SM"), ind(c("TB", 16, TW), w("OU")), c(ld, 0, 256), A.add)
        ts(w("SH"), w("SM"), 1, A.arith_shift_right)
        scatter(c("TB", 16, TW), w("OU"), w("SH"))

    def first_half(cl):
        for i in (0, 1):
            act(c("Q", 512 * i, 512 * i + 512), ind(items(), c("OFF%d" % cl, 32 * i, 32 * i + 32)), F.Copy)
        gather_x(cl, 1, "S")
        marked_gather(1)
        gather_x(cl, 2, "S")
        gather_x(cl, 3, "S")
        lift(0)
        lift(1)
        weave((), marked(0))
        sum_u(0, 0)
        balances(0)
        odd_amounts(0)

    def first_half_0():
        gather_mx(0, "S")
        class_0_lines()
        gather_mx(1, "V")
        gather_x(0, 0, "S")
        balances(0)
        gather_mx(2, "S")
        gather_x(0, 1, "V")
        gather_x(0, 2, "S")
        lift(0)
        lift(1)
        ts(w("SG0"), w("M2"), 32.0, A.mult, 65536.0, A.add)
        ts(w("N256"), w("IDN"), -256.0, A.mult)
        ts(w("BS"), w("BS"), pr, A.add)
        cp(w("CL"), w("IC"))
        act(c("SP", 256, 512), w("KC"), F.Copy)
        sum_u(0, 0)
        gather_x(0, 3, "S")
        lines_to_psum(0, True)
        odd_amounts(0)
        gather_mx(3, "V")

    class_0()
    total = 0
    for t in range(ROUNDS):
        cl, nx = t % 2, 1 - t % 2
        bank = [c("XP", 512 * b, 512 * b + 512) for b in range(4)]
        if t:
            first_half(cl)
        else:
            first_half_0()
        sum_u(0, 1)
        lift(2)
        over(0, "V")
        over(1, "S")
        if t:
            weave((1, 1, 1, 0, 1), hashes(0), marked(2))
            lift(3)
            weave((), marked(3))
        else:
            marks_out(1)
            row_masks(8, 16)
            lift(3)
            weave((), hashes(0))
        count_over(0)
        count_over(1)
        sum_u(1, 0)
        far(0)
        gate(0, 128)
        far(1)
        balances(1)
        odd_amounts(1)
        sum_u(1, 1)
        for b in range(4):
            minus(b, bank[b])
        over(2, "S")
        weave((1, 0, 0, 2, 0, 2, 0), hashes(1), low_keys(0), marks_in(1) if t == 0 else [lambda: None] * 2)
        for b in range(4):
            sign_psum(b, bank[b])
        diff(2)
        count_over(2)
        score(0)
        score(1)
        gate(128, 192)
        sign(2, "S")
        over(3, "S")
        diff(3)
        sign(3, "V")
        if t == 0:
            fill(c("MB1", 15, 256, 16), 4096.0)
        score(2)
        weave((0, 1, 0), keys(cl, c("SP", 0, 128), 0, 128), low_keys(1))
        score(3)
        count_over(3)
        gate(192, 256)
        if t + 1 < ROUNDS:
            masks_of(nx, range(PRE))
        weave((0, 0, 1, 0, 1, 0, 1, 1), keys(cl, scores(2), 128, 192), keys(cl, scores(3), 192, 256))
        winners(t)
        total += send(t)
        moves()
        if t == 0:
            class_1_lines()
        weave((1, 0, 1, 0, 1, 0, 1), *((kappa(), flips(cl, nx)) if t + 1 < ROUNDS else ([lambda: None] * 3, flips(cl, None))))
        if t + 1 < ROUNDS:
            masks_of(nx, range(4, 8))
            lines_to_psum(nx, False)
            fused_list(nx)
        if t + 2 < ROUNDS:
            renew(cl)
        else:
            last(cl)
        if t + 2 == ROUNDS:
            out_columns(cl)
        apply(t)
    dma("Y", "d5", T.yx[:], items())
    out_columns(cl)
    dma("S", "d3", T.ym[:], w("YMB"))
    dma("S", "d4", T.yl[:], w("YLB"))
    for d in ("d3", "d4", "d5"):
        g.sync.wait_ge(T.sem[d], 16)
    g.wait_ge(T.sem.loc, total)
    for q in ("V", "S", "P", "G"):
        g.wait_ge(T.sem["q" + q], seq[q])
    for d in ("d0", "d1", "d2"):
        g.wait_ge(T.sem[d], 16)
